import numpy as np
import ml_dtypes


def mxq(x, axis, fmt="e4m3"):
    dtype, down = {"e4m3": (ml_dtypes.float8_e4m3fn, 7), "e5m2": (ml_dtypes.float8_e5m2, 14)}[fmt]
    v = np.moveaxis(np.asarray(x, np.float32).astype(ml_dtypes.bfloat16).astype(np.float64), axis, -1)
    blocks = v.reshape(v.shape[:-1] + (-1, 32))
    amax = np.abs(blocks).max(-1, keepdims=True)
    byte = np.maximum(np.where(amax > 0, np.frexp(amax)[1] - 1 + 127, 0) - down, 1)
    scale = np.exp2(byte - 127.0)
    codes = (blocks / scale).astype(np.float32).astype(dtype).astype(np.float64)
    return np.moveaxis((codes * scale).reshape(v.shape), -1, axis)


WIDE = False


def mx_kscale(k):
    if not WIDE:
        return np.ones(k)
    levels = np.array([10, -10, 5, -5, 0])
    if k % 512:
        return np.exp2(np.random.permutation(np.resize(levels, k // 32))).repeat(32)
    a = np.empty((k // 512, 16))
    for p in range(k // 512):
        a[p, :8] = np.random.permutation(np.resize(levels, 8))
        for g in range(8):
            far = levels[np.abs(levels - a[p, g]) >= 10]
            a[p, g + 8] = far[np.random.randint(len(far))]
    return np.exp2(a.ravel()).repeat(32)


BF16 = ml_dtypes.bfloat16


def bf(x):
    return np.asarray(x, np.float32).astype(BF16)


def f64(x):
    return np.asarray(x).astype(np.float64)


N, D, P = 1024, 512, 1536


def sigmoid(z):
    return 1.0 / (1.0 + np.exp(-z))


def draw0():
    s, r = mx_kscale(D), mx_kscale(P)
    return {
        "ker": bf(np.random.standard_normal((N, D)) * s),
        "feat": bf(np.random.standard_normal((P, D)) / s),
        "bias": bf(np.random.standard_normal(N) * 0.4),
        "ga": bf(np.exp(0.5 * np.random.standard_normal(P)) * r),
        "gb": bf(np.exp(0.5 * np.random.standard_normal(P)) / r),
        "score": bf(np.random.uniform(0.2, 1.0, N)),
    }


def soft_masks(ker, feat, bias):
    logits = (mxq(ker, 1, "e4m3") @ mxq(feat, 1, "e4m3").T) / np.sqrt(D)
    return np.tanh(logits + bias[:, None])


def tanimoto(u, v):
    x = (mxq(u, 1, "e4m3") @ mxq(v, 1, "e4m3").T) / P
    area = np.mean(u * v, axis=1)
    return x / (area[:, None] + area[None, :] - x)


def core(ker, feat, bias, ga, gb, score):
    sc = f64(score)
    t = soft_masks(f64(ker), f64(feat), f64(bias))
    u = t * f64(ga)[None, :]
    v = t * f64(gb)[None, :]
    iou = tanimoto(u, v)
    gate = sigmoid(8.0 * (sc[:, None] - sc[None, :]))
    return sc[None, :] * np.exp(-256.0 * gate * np.square(iou))


def e4m3fn_bytes(y):
    return np.clip(np.asarray(y, np.float64), -448.0, 448.0).astype(np.float32).astype(ml_dtypes.float8_e4m3fn).view(np.uint8)


def e4m3fn_values(b):
    return np.asarray(b, np.uint8).view(ml_dtypes.float8_e4m3fn).astype(np.float64)


def setup_inputs():
    d = draw0()
    x0 = np.asarray(d['feat']).astype(np.float64)
    s = (np.max(np.abs(x0), axis=(0,), keepdims=True) / 448.0).astype(np.float32)
    out = {}
    for k, v in d.items():
        if k == 'feat':
            out['feat_bytes'] = e4m3fn_bytes(x0 / s.astype(np.float64))
            out['feat_scale'] = s
        else:
            out[k] = v
    return out


def reference(ker, feat_bytes, feat_scale, bias, ga, gb, score):
    return core(ker, e4m3fn_values(feat_bytes) * feat_scale.astype(np.float64), bias, ga, gb, score)

@@ -1,0 +1,399 @@
+from contextlib import ExitStack
+
+import concourse.mybir as mybir
+from concourse.masks import make_identity
+
+N, D, PX = 1024, 512, 1536
+P = 128
+J = 4
+NB = N // P
+NG = PX // (P * J)
+NQ = NB // 2
+
+F32 = mybir.dt.float32
+BF16 = mybir.dt.bfloat16
+U32 = mybir.dt.uint32
+U8 = mybir.dt.uint8
+FP8 = mybir.dt.float8_e4m3fn
+FP8X4 = mybir.dt.float8_e4m3fn_x4
+ACT = mybir.ActivationFunctionType
+ALU = mybir.AluOpType
+
+FLOPS = 2 * N * PX * D + 2 * N * N * PX
+GAIN_N = 32
+HEAD = "COLS W.0.0 W.0.1 W.0.2 W.0.3 KT.0 G.1 KC.0 W.1.1 FT.0.0 FT.0.1 FC.0.0 FC.0.1 G.0 W.1.0 W.1.2 FT.1.0 FC.1.0 FQ.0 G.3 KQ.0 L.0 L.1 TH.0 VQ.0 G.2 W.2.1 TH.1 W.2.3 W.2.2 W.1.3 TR.0 FT.1.1 TR.1 S.0 FC.1.1 W.2.0 U.0 S.1 FQ.1 FT.2.0 L.2 GAB V.0 FC.2.0 U.1 TH.2 V.1 UQ.1 FT.2.1 VQ.1 FC.2.1 L.3 TH.3 KT.1 TR.2 FQ.2 UQ.0 KC.1 S.2 KQ.1"
+LAG = {"order": ('AR', 'KT', 'G', 'M', 'L', 'U', 'TH', 'TR', 'S', 'KQ', 'AO', 'KC', 'SP', 'X', 'SC'), "L": 4, "TH": 3, "TR": 2, "S": 1, "AR": 4, "KT": (2, 7), "KC": (5, 9), "KQ": (6, 13), "AO": (10, 16), "SP": (14, 18), "SC": (15, 19), "G": lambda k: k >= 11 and k % 3 != 0, "X": -2, "XA": 3, "defer": 16, "OL": 3, "late": ((2, 3), (3, 4)), "M": -7, "MA": 1}
+Y2_ACT = lambda k: k % 4 == 1
+G_POOL = lambda k: True
+SJ_POOL = lambda k: False
+
+
+def tile_dynamickernelmasksoftnms_kernel(tc, ker, feat_bytes, feat_scale, bias, ga, gb, score, out):
+    nc = tc.nc
+    with ExitStack() as ctx:
+        keep = ctx.enter_context(tc.tile_pool(name="keep", bufs=1))
+        work = ctx.enter_context(tc.tile_pool(name="work", bufs=3))
+        psum = ctx.enter_context(tc.psum_pool(name="psum", bufs=3))
+        psum_area = ctx.enter_context(tc.psum_pool(name="psum_area", bufs=2))
+        ctx.enter_context(tc.manual_schedule())
+
+        scale_bc = keep.tile([P, D], F32, name="scale_bc")
+        nc.scalar.dma_start(out=scale_bc[:], in_=feat_scale.rearrange("o k -> (o k)").partition_broadcast(P))
+        feat_raw = [keep.tile([P, J, D], U8, name=f"feat_raw{g}") for g in range(NG)]
+        ker_raw = [keep.tile([P, 2, D], BF16, name=f"ker_raw{q}") for q in range(NQ)]
+
+        def load_feat(g):
+            nc.sync.dma_start(out=feat_raw[g][:], in_=feat_bytes[g * 512 : (g + 1) * 512, :].rearrange("(m j) k -> m j k", j=J))
+
+        def load_ker(q):
+            nc.sync.dma_start(out=ker_raw[q][:], in_=ker[q * 256 : (q + 1) * 256, :].rearrange("(b p) k -> p b k", p=P))
+
+        load_feat(0)
+        load_ker(0)
+        rows = keep.tile([P, P], BF16, name="rows")
+        nc.vector.memset(rows[:], 0.0)
+        nc.scalar.dma_start(out=rows[0:NB, :], in_=bias.rearrange("(b p) -> b p", p=P))
+        nc.scalar.dma_start(out=rows[NB : 2 * NB, :], in_=score.rearrange("(b p) -> b p", p=P))
+        score_bc = keep.tile([P, N], BF16, name="score_bc")
+        nc.scalar.dma_start(out=score_bc[:], in_=score.partition_broadcast(P))
+        load_feat(1)
+        load_feat(2)
+        warm = keep.tile([P, 1], F32, name="warm")
+        nc.vector.memset(warm[:], 0.0)
+        ident = keep.tile([P, P], F32, name="ident")
+        make_identity(nc, ident[:])
+        ident_bf = keep.tile([P, P], BF16, name="ident_bf")
+        nc.gpsimd.tensor_copy(out=ident_bf[:], in_=ident[:])
+        nc.scalar.activation(out=warm[:], in_=warm[:], func=ACT.Sigmoid)
+        gains_a = keep.tile([P, NG, J], BF16, name="gains_a")
+        gains_b = keep.tile([P, NG, J], BF16, name="gains_b")
+        nc.sync.dma_start(out=gains_a[:], in_=ga.rearrange("(g m j) -> m g j", m=P, j=J))
+        nc.sync.dma_start(out=gains_b[:], in_=gb.rearrange("(g m j) -> m g j", m=P, j=J))
+        for q in range(1, NQ):
+            load_ker(q)
+
+        gab = keep.tile([P, NG, J], F32, name="gab")
+        cols = keep.tile([P, 2 * NB], F32, name="cols")
+        score8 = keep.tile([P, NB], F32, name="score8")
+        feat_codes = keep.tile([P, PX], U32, name="feat_codes", align_bytes=64)
+        feat_scales = keep.tile([P, PX], U8, name="feat_scales", align_bytes=64)
+        ker_codes = keep.tile([P, N], U32, name="ker_codes", align_bytes=64)
+        ker_scales = keep.tile([P, N], U8, name="ker_scales", align_bytes=64)
+        feat_wide = [keep.tile([P, J, D], BF16, name=f"feat_wide{g}") for g in range(NG)]
+        feat_grouped = [keep.tile([P, J * P, J], BF16, name=f"feat_grouped{g}", align_bytes=64) for g in range(NG)]
+        ker_grouped = [keep.tile([P, 2 * P, J], BF16, name=f"ker_grouped{q}", align_bytes=64) for q in range(NQ)]
+        u_codes = keep.tile([P, NG, N], U32, name="u_codes", align_bytes=64)
+        u_scales = keep.tile([P, NG, N], U8, name="u_scales", align_bytes=64)
+        v_codes = keep.tile([P, NG, N], U32, name="v_codes", align_bytes=64)
+        v_scales = keep.tile([P, NG, N], U8, name="v_scales", align_bytes=64)
+        area_col = keep.tile([P, NB], F32, name="area_col")
+        area_bc = keep.tile([P, N], F32, name="area_bc")
+        gate = keep.tile([P, NB, N], F32, name="gate")
+
+        banks = {}
+
+        def words_in(key, slots, tag):
+            bank = psum.tile([P, 2, 2, P], F32, name="turned", tag=tag)
+            banks[key] = bank
+            for s, x in enumerate(slots):
+                words = x.bitcast(F32)
+                for u in range(2):
+                    nc.tensor.transpose(bank[:, s, u, :], words[:, u : D // 2 : 2], ident[:])
+
+        def words_out(key, grouped, first):
+            dst = grouped[:].rearrange("p n j -> p (n j)").bitcast(F32)[:, first * 2 : (first + 2 * P) * 2]
+            nc.scalar.copy(out=dst.rearrange("p (s r u) -> p s r u", s=2, u=2), in_=banks[key][:].rearrange("p s u r -> p s r u"))
+
+        def W(g, j):
+            nc.vector.tensor_tensor(out=feat_wide[g][:, j, :], in0=feat_raw[g][:, j, :].bitcast(FP8), in1=scale_bc[:], op=ALU.mult)
+
+        def FT(g, half):
+            w = feat_wide[g]
+            words_in(("f", g, half), [w[:, 2 * half, :], w[:, 2 * half + 1, :]], "bank_l")
+
+        def FC(g, half):
+            words_out(("f", g, half), feat_grouped[g], 2 * half * P)
+
+        def FQ(g):
+            s = slice(g * 512, (g + 1) * 512)
+            nc.vector.quantize_mx(out=feat_codes[:, s].bitcast(FP8X4), scales=feat_scales[:, s], in_=feat_grouped[g][:].rearrange("p n j -> p (n j)"))
+
+        def KT(q):
+            words_in(("k", q), [ker_raw[q][:, 0, :], ker_raw[q][:, 1, :]], "bank_l")
+
+        def KC(q):
+            words_out(("k", q), ker_grouped[q], 0)
+
+        def KQ(q):
+            s = slice(q * 256, (q + 1) * 256)
+            nc.vector.quantize_mx(out=ker_codes[:, s].bitcast(FP8X4), scales=ker_scales[:, s], in_=ker_grouped[q][:].rearrange("p n j -> p (n j)"))
+
+        units = [(b, g) for g in range(NG) for b in range(2)] + [(b, g) for b in range(2, NB) for g in range(NG)]
+        area_order = [(b, g) for b in range(NB) for g in range(NG)]
+        unit_of = {bg: k for k, bg in enumerate(units)}
+        nu = len(units)
+        logits, ts, turned, t2s, us, vs, area_ps, spread_ps = {}, {}, {}, {}, {}, {}, {}, {}
+
+        def L(k):
+            b, g = units[k]
+            n, px = slice(b * P, (b + 1) * P), slice(g * 512, (g + 1) * 512)
+            x = psum.tile([P, D], F32, name="logits", tag="bank_l")
+            logits[k] = x
+            nc.tensor.matmul_mx(
+                out=x[:],
+                lhsT=ker_codes[:, n].bitcast(FP8X4),
+                lhsT_scale=ker_scales[:, n],
+                rhs=feat_codes[:, px].bitcast(FP8X4),
+                rhs_scale=feat_scales[:, px],
+                start=True,
+                stop=True,
+            )
+
+        def TH(k):
+            b, g = units[k]
+            t = work.tile([P, D], F32, name="t", bufs=3)
+            ts[k] = t
+            nc.scalar.activation(out=t[:], in_=logits[k][:], func=ACT.Tanh, bias=cols[:, b : b + 1], scale=D**-0.5)
+
+        def TR(k):
+            x = psum.tile([P, J, P], F32, name="t_turned", tag="bank_t")
+            turned[k] = x
+            for j in range(J):
+                nc.tensor.transpose(x[:, j, :], ts[k][:, j * P : (j + 1) * P], ident[:])
+
+        def gain(k, gains, store, name):
+            b, g = units[k]
+            half = b % 2
+            if half == 0:
+                w = work.tile([P, 2 * P, J], BF16, name=name, bufs=5, align_bytes=64)
+                store[b // 2, g] = w
+            nc.vector.tensor_tensor(
+                out=store[b // 2, g][:, half * P : (half + 1) * P, :],
+                in0=turned[k][:].rearrange("p j n -> p n j"),
+                in1=gains[:, g, :].unsqueeze(1).to_broadcast([P, P, J]),
+                op=ALU.mult,
+            )
+
+        def quant(k, codes, scales, store):
+            b, g = units[k]
+            if b % 2 == 0:
+                return
+            s = slice((b - 1) * P, (b + 1) * P)
+            nc.vector.quantize_mx(out=codes[:, g, s].bitcast(FP8X4), scales=scales[:, g, s], in_=store[b // 2, g][:].rearrange("p n j -> p (n j)"))
+
+        def U(k):
+            gain(k, gains_a, us, "u")
+
+        def V(k):
+            gain(k, gains_b, vs, "v")
+
+        def UQ(k):
+            quant(k, u_codes, u_scales, us)
+
+        def VQ(k):
+            quant(k, v_codes, v_scales, vs)
+
+        def S(k):
+            t2 = work.tile([P, J, P], F32, name="t2", bufs=8)
+            t2s[k] = t2
+            nc.scalar.activation(out=t2[:], in_=turned[k][:], func=ACT.Square)
+
+        def AR(n):
+            b, g = area_order[n]
+            if b % 2 == 0 and g == 0:
+                acc = psum_area.tile([P, 2, GAIN_N], F32, name="area_acc", tag="area_acc")
+                area_ps[b // 2] = acc
+            for j in range(J):
+                nc.tensor.matmul(
+                    out=area_ps[b // 2][:, b % 2, :],
+                    lhsT=t2s[unit_of[b, g]][:, j, :],
+                    rhs=gab[:, g, j : j + 1].to_broadcast([P, GAIN_N]),
+                    start=(g == 0 and j == 0),
+                    stop=(g == NG - 1 and j == J - 1),
+                )
+
+        def AO(q):
+            nc.vector.tensor_copy(out=area_col[:, 2 * q : 2 * q + 2], in_=area_ps[q][:, :, 0])
+
+        def SP(q):
+            pool, tag = (psum, "bank_l") if q < 2 else (psum_area, "area_acc")
+            bank = pool.tile([P, 2, P], F32, name="spread", tag=tag)
+            spread_ps[q] = bank
+            for h in range(2):
+                b = 2 * q + h
+                nc.tensor.matmul(out=bank[:, h, :], lhsT=area_col[:, b : b + 1].to_broadcast([P, P]), rhs=ident[:], start=True, stop=True)
+
+        def SC(q):
+            nc.scalar.copy(out=area_bc[:, q * 256 : (q + 1) * 256], in_=spread_ps[q][:].rearrange("p b n -> p (b n)"))
+
+        g_done, gm_done = set(), set()
+
+        def G(n):
+            i, h = divmod(n, 2)
+            g_done.add(n)
+            nc.scalar.activation(out=gate[:, i, h * 512 : (h + 1) * 512], in_=score_bc[:, h * 512 : (h + 1) * 512], func=ACT.Sigmoid, bias=score8[:, i : i + 1], scale=-8.0)
+
+        def COLS():
+            cols_ps = psum.tile([P, P], BF16, name="cols_ps", tag="bank_t")
+            nc.tensor.transpose(cols_ps[:], rows[:], ident_bf[:])
+            nc.scalar.copy(out=cols[:], in_=cols_ps[:, 0 : 2 * NB])
+            nc.scalar.activation(out=score8[:], in_=cols_ps[:, NB : 2 * NB], func=ACT.Copy, scale=8.0)
+
+        def GAB():
+            nc.vector.tensor_tensor(out=gab[:], in0=gains_a[:], in1=gains_b[:], op=ALU.mult)
+
+        halves = [(i, h) for h in range(2) for i in range(NB)]
+        nh = len(halves)
+        xs, ms, ds, rs, ys, y2s, es = {}, {}, {}, {}, {}, {}, {}
+
+        def X(k):
+            i, h = halves[k]
+            x = psum.tile([P, 512], F32, name="x", tag=("bank_l", "bank_t")[k % 2])
+            xs[k] = x
+            for g in range(NG):
+                nc.tensor.matmul_mx(
+                    out=x[:],
+                    lhsT=u_codes[:, g, i * P : (i + 1) * P].bitcast(FP8X4),
+                    lhsT_scale=u_scales[:, g, i * P : (i + 1) * P],
+                    rhs=v_codes[:, g, h * 512 : (h + 1) * 512].bitcast(FP8X4),
+                    rhs_scale=v_scales[:, g, h * 512 : (h + 1) * 512],
+                    start=(g == 0),
+                    stop=(g == NG - 1),
+                )
+
+        def M(k):
+            i, h = halves[k]
+            m = work.tile([P, 512], F32, name="m")
+            ms[k] = m
+            nc.vector.tensor_tensor(out=m[:], in0=area_bc[:, h * 512 : (h + 1) * 512], in1=xs[k][:], op=ALU.subtract)
+
+        def D2(k):
+            i, h = halves[k]
+            d2 = work.tile([P, 512], F32, name="d2")
+            ds[k] = d2
+            nc.scalar.activation(out=d2[:], in_=ms[k][:], func=ACT.Square, bias=area_col[:, i : i + 1])
+
+        def R(k):
+            r = work.tile([P, 512], F32, name="r")
+            rs[k] = r
+            nc.scalar.activation(out=r[:], in_=ds[k][:], func=ACT.Abs_reciprocal_sqrt)
+
+        def Y(k):
+            y = work.tile([P, 512], F32, name="y")
+            ys[k] = y
+            nc.vector.tensor_tensor(out=y[:], in0=xs[k][:], in1=rs[k][:], op=ALU.mult)
+
+        def Y2(k):
+            y2 = work.tile([P, 512], F32, name="y2")
+            y2s[k] = y2
+            if Y2_ACT(k):
+                nc.scalar.activation(out=y2[:], in_=ys[k][:], func=ACT.Square)
+            else:
+                nc.vector.tensor_tensor(out=y2[:], in0=ys[k][:], in1=ys[k][:], op=ALU.mult)
+
+        def GM(k):
+            i, h = halves[k]
+            s = slice(h * 512, (h + 1) * 512)
+            eng = nc.gpsimd if G_POOL(k) else nc.vector
+            assert g_done >= {2 * i + h}
+            gm_done.add(k)
+            eng.tensor_tensor(out=gate[:, i, s], in0=y2s[k][:], in1=gate[:, i, s], op=ALU.mult)
+
+        def E(k):
+            i, h = halves[k]
+            assert k in gm_done
+            e = work.tile([P, 512], F32, name="e", bufs=4)
+            es[k] = e
+            nc.scalar.activation(out=e[:], in_=gate[:, i, h * 512 : (h + 1) * 512], func=ACT.Exp, scale=-256.0)
+
+        def O(k):
+            i, h = halves[k]
+            s = slice(h * 512, (h + 1) * 512)
+            o = work.tile([P, 512], F32, name="o", bufs=6)
+            eng = nc.gpsimd if SJ_POOL(k) else nc.vector
+            eng.tensor_tensor(out=o[:], in0=es[k][:], in1=score_bc[:, s], op=ALU.mult)
+            nc.sync.dma_start(out=out[i * P : (i + 1) * P, s], in_=o[:])
+
+        calls = {"W": W, "FT": FT, "FC": FC, "FQ": FQ, "KT": KT, "KC": KC, "KQ": KQ, "L": L, "TH": TH, "TR": TR, "U": U, "V": V, "UQ": UQ, "VQ": VQ, "S": S, "AR": AR, "G": G, "COLS": COLS, "GAB": GAB}
+        done = {}
+        for item in HEAD.split():
+            name, *args = item.split(".")
+            args = [int(a) for a in args]
+            calls[name](*args)
+            if len(args) == 1:
+                done[name] = max(done.get(name, -1), args[0])
+
+        def upto(fn, name, k, last):
+            while done.get(name, -1) < min(k, last - 1):
+                done[name] = done.get(name, -1) + 1
+                fn(done[name])
+
+        first = done.get("U", -1) + 1
+        for k in range(first, nu + 1):
+            for item in LAG["order"]:
+                if item == "L":
+                    upto(L, "L", k + LAG["L"], nu)
+                elif item == "TH":
+                    upto(TH, "TH", k + LAG["TH"], nu)
+                elif item == "TR":
+                    upto(TR, "TR", k + LAG["TR"], nu)
+                elif item == "S":
+                    upto(S, "S", k + LAG["S"], nu)
+                elif item == "AR":
+                    upto(AR, "AR", k - LAG["AR"], nu)
+                elif item == "U":
+                    upto(U, "U", k, nu)
+                    upto(UQ, "UQ", k - 1, nu)
+                    upto(V, "V", k, nu)
+                    upto(VQ, "VQ", k - 1, nu)
+                elif item == "KT" and k in LAG["KT"]:
+                    KT(LAG["KT"].index(k) + 2)
+                elif item == "KC" and k in LAG["KC"]:
+                    KC(LAG["KC"].index(k) + 2)
+                elif item == "KQ" and k in LAG["KQ"]:
+                    KQ(LAG["KQ"].index(k) + 2)
+                elif item == "AO" and k in LAG["AO"]:
+                    AO(LAG["AO"].index(k))
+                elif item == "SP" and k in LAG["SP"]:
+                    SP(LAG["SP"].index(k))
+                elif item == "SC" and k in LAG["SC"]:
+                    SC(LAG["SC"].index(k))
+                elif item == "G" and LAG["G"](k):
+                    upto(G, "G", done["G"] + 1, 2 * NB)
+                elif item == "X":
+                    upto(X, "X", k - nu + LAG["X"], nh)
+                elif item == "M":
+                    upto(M, "M", k - nu + LAG["M"], nh)
+        upto(G, "G", 2 * NB - 1, 2 * NB)
+        for k in range(-1, nh + 4):
+            if k <= LAG["AR"] - 2:
+                upto(AR, "AR", nu - LAG["AR"] + k + 1, nu)
+            upto(X, "X", k + LAG["XA"], nh)
+            upto(M, "M", k + LAG["MA"], nh)
+            for q, at in LAG["late"]:
+                if k == at:
+                    AO(q)
+                if k == at + 1:
+                    SP(q)
+                if k == at + 2:
+                    SC(q)
+            if 0 <= k < nh:
+                D2(k)
+            if 0 <= k - 1 < nh:
+                R(k - 1)
+            if 0 <= k - 2 < nh:
+                Y(k - 2)
+            if 0 <= k - 3 < LAG["defer"]:
+                Y2(k - 3)
+            if 0 <= k - 4 < LAG["defer"]:
+                GM(k - 4)
+        nxt = LAG["defer"]
+        for k in range(nh + LAG["OL"]):
+            if k < nh:
+                E(k)
+            if nxt < nh:
+                Y2(nxt)
+                GM(nxt)
+                nxt += 1
+            if k >= LAG["OL"]:
+                O(k - LAG["OL"])

@@ -21,11 +21,16 @@ ALU = mybir.AluOpType
 
 FLOPS = 2 * N * PX * D + 2 * N * N * PX
 GAIN_N = 32
-HEAD = "COLS W.0.0 W.0.1 W.0.2 W.0.3 KT.0 G.1 KC.0 W.1.1 FT.0.0 FT.0.1 FC.0.0 FC.0.1 G.0 W.1.0 W.1.2 FT.1.0 FC.1.0 FQ.0 G.3 KQ.0 L.0 L.1 TH.0 VQ.0 G.2 W.2.1 TH.1 W.2.3 W.2.2 W.1.3 TR.0 FT.1.1 TR.1 S.0 FC.1.1 W.2.0 U.0 S.1 FQ.1 FT.2.0 L.2 GAB V.0 FC.2.0 U.1 TH.2 V.1 UQ.1 FT.2.1 VQ.1 FC.2.1 L.3 TH.3 KT.1 TR.2 FQ.2 UQ.0 KC.1 S.2 KQ.1"
-LAG = {"order": ('AR', 'KT', 'G', 'M', 'L', 'U', 'TH', 'TR', 'S', 'KQ', 'AO', 'KC', 'SP', 'X', 'SC'), "L": 4, "TH": 3, "TR": 2, "S": 1, "AR": 4, "KT": (2, 7), "KC": (5, 9), "KQ": (6, 13), "AO": (10, 16), "SP": (14, 18), "SC": (15, 19), "G": lambda k: k >= 11 and k % 3 != 0, "X": -2, "XA": 3, "defer": 16, "OL": 3, "late": ((2, 3), (3, 4)), "M": -7, "MA": 1}
-Y2_ACT = lambda k: k % 4 == 1
-G_POOL = lambda k: True
-SJ_POOL = lambda k: False
+HEAD = "W.0.0 W.0.1 FT.0.0 W.1.2 W.0.2 FC.0.0 KT.0 W.0.3 FT.0.1 FC.0.1 KC.0 KQ.0 W.1.0 FQ.0 W.1.1 SB.0 COLS SBC.0 SB.1 L.0 G.0 GAB TH.0 W.1.3 FT.1.0 W.2.2 FC.1.0 SBC.1 FT.1.1 L.1 FC.1.1 UQ.0 TH.1 VQ.0 W.2.3 TR.0 G.1 S.0 W.2.0 FQ.1 FT.2.1 TR.1 W.2.1 FT.2.0 U.0 L.3 G.3 S.1 L.2 TH.2 FC.2.0 KT.1 V.0 TH.3 KC.1 FC.2.1 U.1 FQ.2 V.1 KQ.1 TR.2 VQ.1 S.2 UQ.1 G.2"
+LAG = {"order": ('KT', 'SC', 'L', 'M', 'AO', 'AR', 'TH', 'TR', 'S', 'G', 'KC', 'KQ', 'U', 'X', 'SP'), "L": 4, "TH": 3, "TR": 2, "S": 1, "AR": 4, "KT": (2, 7), "KC": (5, 8), "KQ": (7, 12), "AO": (12, 17), "SP": (15, 18), "SC": (17, 20), "G": lambda k: k >= 7 and k % 3 != 0, "X": 4, "XA": 2, "defer": 16, "OL": 2, "late": ((2, 3), (3, 4)), "M": 2, "MA": 1, "R": 1, "Y": 2, "Y2": 3, "GM": 4}
+D2_ENG = "aapaapaapaaaaapa"
+Y2_ENG = "aaaaaaaadaaaaada"
+GM_ENG = "pppdpdpppdddpdpd"
+SJ_ENG = "dddddddddddddddd"
+CAST_ENG = "ddaaadpddppp"
+KC_ENG = "aaad"
+SC_ENG = "addd"
+SBC_ENG = "aa"
 
 
 def tile_dynamickernelmasksoftnms_kernel(tc, ker, feat_bytes, feat_scale, bias, ga, gb, score, out):
@@ -37,8 +42,6 @@ def tile_dynamickernelmasksoftnms_kernel(tc, ker, feat_bytes, feat_scale, bias, 
         psum_area = ctx.enter_context(tc.psum_pool(name="psum_area", bufs=2))
         ctx.enter_context(tc.manual_schedule())
 
-        scale_bc = keep.tile([P, D], F32, name="scale_bc")
-        nc.scalar.dma_start(out=scale_bc[:], in_=feat_scale.rearrange("o k -> (o k)").partition_broadcast(P))
         feat_raw = [keep.tile([P, J, D], U8, name=f"feat_raw{g}") for g in range(NG)]
         ker_raw = [keep.tile([P, 2, D], BF16, name=f"ker_raw{q}") for q in range(NQ)]
 
@@ -54,8 +57,9 @@ def tile_dynamickernelmasksoftnms_kernel(tc, ker, feat_bytes, feat_scale, bias, 
         nc.vector.memset(rows[:], 0.0)
         nc.scalar.dma_start(out=rows[0:NB, :], in_=bias.rearrange("(b p) -> b p", p=P))
         nc.scalar.dma_start(out=rows[NB : 2 * NB, :], in_=score.rearrange("(b p) -> b p", p=P))
-        score_bc = keep.tile([P, N], BF16, name="score_bc")
-        nc.scalar.dma_start(out=score_bc[:], in_=score.partition_broadcast(P))
+        score_bc = keep.tile([P, N], F32, name="score_bc")
+        scale4 = keep.tile([P, J], F32, name="scale4")
+        nc.scalar.dma_start(out=scale4[:], in_=feat_scale.rearrange("o (p t) -> p (o t)", p=P, t=J))
         load_feat(1)
         load_feat(2)
         warm = keep.tile([P, 1], F32, name="warm")
@@ -93,26 +97,37 @@ def tile_dynamickernelmasksoftnms_kernel(tc, ker, feat_bytes, feat_scale, bias, 
         banks = {}
 
         def words_in(key, slots, tag):
-            bank = psum.tile([P, 2, 2, P], F32, name="turned", tag=tag)
+            bank = psum.tile([P, 2, 2 * P], F32, name="turned", tag=tag)
             banks[key] = bank
             for s, x in enumerate(slots):
                 words = x.bitcast(F32)
                 for u in range(2):
-                    nc.tensor.transpose(bank[:, s, u, :], words[:, u : D // 2 : 2], ident[:])
+                    nc.tensor.transpose(bank[:, u, s * P : (s + 1) * P], words[:, u : D // 2 : 2], ident[:])
 
-        def words_out(key, grouped, first):
-            dst = grouped[:].rearrange("p n j -> p (n j)").bitcast(F32)[:, first * 2 : (first + 2 * P) * 2]
-            nc.scalar.copy(out=dst.rearrange("p (s r u) -> p s r u", s=2, u=2), in_=banks[key][:].rearrange("p s u r -> p s r u"))
+        def copy(e, out, in_):
+            if e == "a":
+                nc.scalar.copy(out=out, in_=in_)
+            elif e == "d":
+                nc.vector.tensor_copy(out=out, in_=in_)
+            else:
+                nc.gpsimd.tensor_copy(out=out, in_=in_)
 
         def W(g, j):
-            nc.vector.tensor_tensor(out=feat_wide[g][:, j, :], in0=feat_raw[g][:, j, :].bitcast(FP8), in1=scale_bc[:], op=ALU.mult)
+            src, dst = feat_raw[g][:, j, :].bitcast(FP8), feat_wide[g][:, j, :]
+            copy(CAST_ENG[g * J + j], dst, src)
 
         def FT(g, half):
             w = feat_wide[g]
             words_in(("f", g, half), [w[:, 2 * half, :], w[:, 2 * half + 1, :]], "bank_l")
 
         def FC(g, half):
-            words_out(("f", g, half), feat_grouped[g], 2 * half * P)
+            first = 2 * half * P
+            nc.vector.tensor_tensor(
+                out=feat_grouped[g][:, first : first + 2 * P, :].rearrange("p n (u e) -> p n u e", u=2),
+                in0=banks["f", g, half][:].bitcast(BF16).rearrange("p u (n e) -> p n u e", e=2),
+                in1=scale4[:].rearrange("p (u e) -> p u e", u=2).unsqueeze(1).to_broadcast([P, 2 * P, 2, 2]),
+                op=ALU.mult,
+            )
 
         def FQ(g):
             s = slice(g * 512, (g + 1) * 512)
@@ -122,7 +137,8 @@ def tile_dynamickernelmasksoftnms_kernel(tc, ker, feat_bytes, feat_scale, bias, 
             words_in(("k", q), [ker_raw[q][:, 0, :], ker_raw[q][:, 1, :]], "bank_l")
 
         def KC(q):
-            words_out(("k", q), ker_grouped[q], 0)
+            dst = ker_grouped[q][:].rearrange("p n j -> p (n j)").bitcast(F32)
+            copy(KC_ENG[q], dst.rearrange("p (r u) -> p r u", u=2), banks["k", q][:].rearrange("p u r -> p r u"))
 
         def KQ(q):
             s = slice(q * 256, (q + 1) * 256)
@@ -224,7 +240,7 @@ def tile_dynamickernelmasksoftnms_kernel(tc, ker, feat_bytes, feat_scale, bias, 
                 nc.tensor.matmul(out=bank[:, h, :], lhsT=area_col[:, b : b + 1].to_broadcast([P, P]), rhs=ident[:], start=True, stop=True)
 
         def SC(q):
-            nc.scalar.copy(out=area_bc[:, q * 256 : (q + 1) * 256], in_=spread_ps[q][:].rearrange("p b n -> p (b n)"))
+            copy(SC_ENG[q], area_bc[:, q * 256 : (q + 1) * 256], spread_ps[q][:].rearrange("p b n -> p (b n)"))
 
         g_done, gm_done = set(), set()
 
@@ -238,6 +254,16 @@ def tile_dynamickernelmasksoftnms_kernel(tc, ker, feat_bytes, feat_scale, bias, 
             nc.tensor.transpose(cols_ps[:], rows[:], ident_bf[:])
             nc.scalar.copy(out=cols[:], in_=cols_ps[:, 0 : 2 * NB])
             nc.scalar.activation(out=score8[:], in_=cols_ps[:, NB : 2 * NB], func=ACT.Copy, scale=8.0)
+
+        def SB(h):
+            bank = psum_area.tile([P, 4, P], F32, name="score_ps", tag="area_acc")
+            banks["s", h] = bank
+            for b in range(4):
+                r = NB + 4 * h + b
+                nc.tensor.matmul(out=bank[:, b, :], lhsT=ident_bf[:, r : r + 1].to_broadcast([P, P]), rhs=rows[:], start=True, stop=True)
+
+        def SBC(h):
+            copy(SBC_ENG[h], score_bc[:, h * 512 : (h + 1) * 512], banks["s", h][:].rearrange("p b n -> p (b n)"))
 
         def GAB():
             nc.vector.tensor_tensor(out=gab[:], in0=gains_a[:], in1=gains_b[:], op=ALU.mult)
@@ -263,18 +289,24 @@ def tile_dynamickernelmasksoftnms_kernel(tc, ker, feat_bytes, feat_scale, bias, 
 
         def M(k):
             i, h = halves[k]
-            m = work.tile([P, 512], F32, name="m")
+            m = work.tile([P, 512], F32, name="m", bufs=4)
             ms[k] = m
-            nc.vector.tensor_tensor(out=m[:], in0=area_bc[:, h * 512 : (h + 1) * 512], in1=xs[k][:], op=ALU.subtract)
+            if D2_ENG[k] == "a":
+                nc.vector.tensor_tensor(out=m[:], in0=area_bc[:, h * 512 : (h + 1) * 512], in1=xs[k][:], op=ALU.subtract)
+            else:
+                nc.vector.scalar_tensor_tensor(out=m[:], in0=xs[k][:], scalar=area_col[:, i : i + 1], in1=area_bc[:, h * 512 : (h + 1) * 512], op0=ALU.subtract, op1=ALU.subtract)
 
         def D2(k):
             i, h = halves[k]
-            d2 = work.tile([P, 512], F32, name="d2")
+            d2 = work.tile([P, 512], F32, name="d2", bufs=4)
             ds[k] = d2
-            nc.scalar.activation(out=d2[:], in_=ms[k][:], func=ACT.Square, bias=area_col[:, i : i + 1])
+            if D2_ENG[k] == "a":
+                nc.scalar.activation(out=d2[:], in_=ms[k][:], func=ACT.Square, bias=area_col[:, i : i + 1])
+            else:
+                nc.gpsimd.tensor_tensor(out=d2[:], in0=ms[k][:], in1=ms[k][:], op=ALU.mult)
 
         def R(k):
-            r = work.tile([P, 512], F32, name="r")
+            r = work.tile([P, 512], F32, name="r", bufs=4)
             rs[k] = r
             nc.scalar.activation(out=r[:], in_=ds[k][:], func=ACT.Abs_reciprocal_sqrt)
 
@@ -286,15 +318,16 @@ def tile_dynamickernelmasksoftnms_kernel(tc, ker, feat_bytes, feat_scale, bias, 
         def Y2(k):
             y2 = work.tile([P, 512], F32, name="y2")
             y2s[k] = y2
-            if Y2_ACT(k):
+            if Y2_ENG[k] == "a":
                 nc.scalar.activation(out=y2[:], in_=ys[k][:], func=ACT.Square)
             else:
-                nc.vector.tensor_tensor(out=y2[:], in0=ys[k][:], in1=ys[k][:], op=ALU.mult)
+                eng = nc.vector if Y2_ENG[k] == "d" else nc.gpsimd
+                eng.tensor_tensor(out=y2[:], in0=ys[k][:], in1=ys[k][:], op=ALU.mult)
 
         def GM(k):
             i, h = halves[k]
             s = slice(h * 512, (h + 1) * 512)
-            eng = nc.gpsimd if G_POOL(k) else nc.vector
+            eng = nc.gpsimd if GM_ENG[k] == "p" else nc.vector
             assert g_done >= {2 * i + h}
             gm_done.add(k)
             eng.tensor_tensor(out=gate[:, i, s], in0=y2s[k][:], in1=gate[:, i, s], op=ALU.mult)
@@ -310,11 +343,11 @@ def tile_dynamickernelmasksoftnms_kernel(tc, ker, feat_bytes, feat_scale, bias, 
             i, h = halves[k]
             s = slice(h * 512, (h + 1) * 512)
             o = work.tile([P, 512], F32, name="o", bufs=6)
-            eng = nc.gpsimd if SJ_POOL(k) else nc.vector
+            eng = nc.gpsimd if SJ_ENG[k] == "p" else nc.vector
             eng.tensor_tensor(out=o[:], in0=es[k][:], in1=score_bc[:, s], op=ALU.mult)
             nc.sync.dma_start(out=out[i * P : (i + 1) * P, s], in_=o[:])
 
-        calls = {"W": W, "FT": FT, "FC": FC, "FQ": FQ, "KT": KT, "KC": KC, "KQ": KQ, "L": L, "TH": TH, "TR": TR, "U": U, "V": V, "UQ": UQ, "VQ": VQ, "S": S, "AR": AR, "G": G, "COLS": COLS, "GAB": GAB}
+        calls = {"W": W, "FT": FT, "FC": FC, "FQ": FQ, "KT": KT, "KC": KC, "KQ": KQ, "L": L, "TH": TH, "TR": TR, "U": U, "V": V, "UQ": UQ, "VQ": VQ, "S": S, "AR": AR, "G": G, "COLS": COLS, "GAB": GAB, "SB": SB, "SBC": SBC}
         done = {}
         for item in HEAD.split():
             name, *args = item.split(".")
@@ -377,16 +410,14 @@ def tile_dynamickernelmasksoftnms_kernel(tc, ker, feat_bytes, feat_scale, bias, 
                     SP(q)
                 if k == at + 2:
                     SC(q)
-            if 0 <= k < nh:
-                D2(k)
-            if 0 <= k - 1 < nh:
-                R(k - 1)
-            if 0 <= k - 2 < nh:
-                Y(k - 2)
-            if 0 <= k - 3 < LAG["defer"]:
-                Y2(k - 3)
-            if 0 <= k - 4 < LAG["defer"]:
-                GM(k - 4)
+            upto(D2, "D2", k, nh)
+            upto(R, "R", k - LAG["R"], nh)
+            upto(Y, "Y", k - LAG["Y"], nh)
+            upto(Y2, "Y2", k - LAG["Y2"], LAG["defer"])
+            upto(GM, "GM", k - LAG["GM"], LAG["defer"])
+        upto(Y, "Y", nh, nh)
+        upto(Y2, "Y2", nh, LAG["defer"])
+        upto(GM, "GM", nh, LAG["defer"])
         nxt = LAG["defer"]
         for k in range(nh + LAG["OL"]):
             if k < nh:

@@ -20,30 +20,32 @@ ACT = mybir.ActivationFunctionType
 ALU = mybir.AluOpType
 
 FLOPS = 2 * N * PX * D + 2 * N * N * PX
-GAIN_N = 32
-HEAD = "W.0.0 W.0.1 FT.0.0 W.1.2 W.0.2 FC.0.0 KT.0 W.0.3 FT.0.1 FC.0.1 KC.0 KQ.0 W.1.0 FQ.0 W.1.1 SB.0 COLS SBC.0 SB.1 L.0 G.0 GAB TH.0 W.1.3 FT.1.0 W.2.2 FC.1.0 SBC.1 FT.1.1 L.1 FC.1.1 UQ.0 TH.1 VQ.0 W.2.3 TR.0 G.1 S.0 W.2.0 FQ.1 FT.2.1 TR.1 W.2.1 FT.2.0 U.0 L.3 G.3 S.1 L.2 TH.2 FC.2.0 KT.1 V.0 TH.3 KC.1 FC.2.1 U.1 FQ.2 V.1 KQ.1 TR.2 VQ.1 S.2 UQ.1 G.2"
-LAG = {"order": ('KT', 'SC', 'L', 'M', 'AO', 'AR', 'TH', 'TR', 'S', 'G', 'KC', 'KQ', 'U', 'X', 'SP'), "L": 4, "TH": 3, "TR": 2, "S": 1, "AR": 4, "KT": (2, 7), "KC": (5, 8), "KQ": (7, 12), "AO": (12, 17), "SP": (15, 18), "SC": (17, 20), "G": lambda k: k >= 7 and k % 3 != 0, "X": 4, "XA": 2, "defer": 16, "OL": 2, "late": ((2, 3), (3, 4)), "M": 2, "MA": 1, "R": 1, "Y": 2, "Y2": 3, "GM": 4}
-D2_ENG = "aapaapaapaaaaapa"
-Y2_ENG = "aaaaaaaadaaaaada"
-GM_ENG = "pppdpdpppdddpdpd"
+GAIN_N = 48
+HEAD = "W.2.2 DM W.0.1 W.0.3 DM DM DM W.0.0 W.0.2 FT.0.0 DM DM FT.0.1 KT.0 FC.0.0 FC.0.1 KC.0 W.1.1 GAB W.1.3 W.1.2 W.2.1 KQ.0 W.1.0 SB.0 COLS DM FT.1.0 DM DM SB.1 SBC.0 W.2.3 W.2.0 FT.1.1 FQ.0 L.0 L.1 SBC.1 FC.1.0 DM TH.0 FC.1.1 FQ.1 G.1 TH.1 FT.2.1 G.0 Q.0 TR.0 FT.2.0 TR.1 S.0 L.2 FC.2.1 L.3 FC.2.0 U.0 DM G.3 TH.2 S.1 TH.3 G.2 DM FQ.2 KT.1 KC.1 DM U.1 TR.2 KQ.1 S.2 Q.1"
+LAG = {"order": ('L', 'M', 'Q', 'AR', 'KC', 'TH', 'KQ', 'TR', 'S', 'X', 'U', 'SP', 'G', 'KT', 'AO', 'SC'), "L": 4, "TH": 3, "TR": 2, "S": 1, "AR": 2, "KT": (3, 4), "KC": (5, 9), "KQ": (7, 10), "AO": (12, 17), "SP": (15, 18), "SC": (21, 19), "G": lambda k: k >= 8 and k % 3 != 0, "X": 4, "XA": 2, "defer": 16, "OL": 0, "late": ((2, 3), (3, 4)), "M": 2, "MA": 1, "R": 1, "Y": 2, "Y2": 3, "GM": 4, "LG": 1, "LP": 0, "TRG": 2, "TRP": 0, "NL": 3, "NT": 3, "AB": 2, "ARR": 4, "T2": 8, "AV": (), "GBC": (), "Q": 2}
+D2_ENG = "apapaaapapaaaaaa"
+Y2_ENG = "daaaaaaapapaaaad"
+GM_ENG = "pppdppdppppdpddd"
 SJ_ENG = "dddddddddddddddd"
-CAST_ENG = "ddaaadpddppp"
+CAST_ENG = "dpdppppdaaaa"
 KC_ENG = "aaad"
 SC_ENG = "addd"
 SBC_ENG = "aa"
+DT = ()
 
 
 def tile_dynamickernelmasksoftnms_kernel(tc, ker, feat_bytes, feat_scale, bias, ga, gb, score, out):
     nc = tc.nc
     with ExitStack() as ctx:
         keep = ctx.enter_context(tc.tile_pool(name="keep", bufs=1))
+        head = ctx.enter_context(tc.tile_pool(name="head", bufs=1))
         work = ctx.enter_context(tc.tile_pool(name="work", bufs=3))
         psum = ctx.enter_context(tc.psum_pool(name="psum", bufs=3))
-        psum_area = ctx.enter_context(tc.psum_pool(name="psum_area", bufs=2))
+        psum_area = ctx.enter_context(tc.psum_pool(name="psum_area", bufs=LAG["AB"]))
         ctx.enter_context(tc.manual_schedule())
 
-        feat_raw = [keep.tile([P, J, D], U8, name=f"feat_raw{g}") for g in range(NG)]
-        ker_raw = [keep.tile([P, 2, D], BF16, name=f"ker_raw{q}") for q in range(NQ)]
+        feat_raw = [head.tile([P, J, D], U8, name=f"feat_raw{g}") for g in range(NG)]
+        ker_raw = [head.tile([P, 2, D], BF16, name=f"ker_raw{q}") for q in range(NQ)]
 
         def load_feat(g):
             nc.sync.dma_start(out=feat_raw[g][:], in_=feat_bytes[g * 512 : (g + 1) * 512, :].rearrange("(m j) k -> m j k", j=J))
@@ -62,6 +64,8 @@ def tile_dynamickernelmasksoftnms_kernel(tc, ker, feat_bytes, feat_scale, bias, 
         nc.scalar.dma_start(out=scale4[:], in_=feat_scale.rearrange("o (p t) -> p (o t)", p=P, t=J))
         load_feat(1)
         load_feat(2)
+        zero = keep.tile([P, 512], BF16, name="zero")
+        nc.vector.memset(zero[:], 0.0)
         warm = keep.tile([P, 1], F32, name="warm")
         nc.vector.memset(warm[:], 0.0)
         ident = keep.tile([P, P], F32, name="ident")
@@ -69,35 +73,37 @@ def tile_dynamickernelmasksoftnms_kernel(tc, ker, feat_bytes, feat_scale, bias, 
         ident_bf = keep.tile([P, P], BF16, name="ident_bf")
         nc.gpsimd.tensor_copy(out=ident_bf[:], in_=ident[:])
         nc.scalar.activation(out=warm[:], in_=warm[:], func=ACT.Sigmoid)
-        gains_a = keep.tile([P, NG, J], BF16, name="gains_a")
-        gains_b = keep.tile([P, NG, J], BF16, name="gains_b")
-        nc.sync.dma_start(out=gains_a[:], in_=ga.rearrange("(g m j) -> m g j", m=P, j=J))
-        nc.sync.dma_start(out=gains_b[:], in_=gb.rearrange("(g m j) -> m g j", m=P, j=J))
+        gains = keep.tile([P, 2, 4, J], BF16, name="gains")
+        for i, v in enumerate((ga, gb)):
+            nc.sync.dma_start(out=gains[:, i, 0:NG, :], in_=v.rearrange("(g m j) -> m g j", m=P, j=J))
         for q in range(1, NQ):
             load_ker(q)
 
-        gab = keep.tile([P, NG, J], F32, name="gab")
+        gab = keep.tile([P, NG, J, GAIN_N], F32, name="gab")
+        if DT:
+            gains_row = [head.tile([P, NG, P, J], BF16, name=f"gains_row{i}") for i in range(2)]
+            gab_bc = keep.tile([P, NG, J, P], F32, name="gab_bc")
+            for i, v in enumerate((ga, gb)):
+                nc.sync.dma_start(out=gains_row[i][:].rearrange("p g m j -> p (g m j)"), in_=v.partition_broadcast(P))
         cols = keep.tile([P, 2 * NB], F32, name="cols")
         score8 = keep.tile([P, NB], F32, name="score8")
         feat_codes = keep.tile([P, PX], U32, name="feat_codes", align_bytes=64)
         feat_scales = keep.tile([P, PX], U8, name="feat_scales", align_bytes=64)
         ker_codes = keep.tile([P, N], U32, name="ker_codes", align_bytes=64)
         ker_scales = keep.tile([P, N], U8, name="ker_scales", align_bytes=64)
-        feat_wide = [keep.tile([P, J, D], BF16, name=f"feat_wide{g}") for g in range(NG)]
-        feat_grouped = [keep.tile([P, J * P, J], BF16, name=f"feat_grouped{g}", align_bytes=64) for g in range(NG)]
-        ker_grouped = [keep.tile([P, 2 * P, J], BF16, name=f"ker_grouped{q}", align_bytes=64) for q in range(NQ)]
-        u_codes = keep.tile([P, NG, N], U32, name="u_codes", align_bytes=64)
-        u_scales = keep.tile([P, NG, N], U8, name="u_scales", align_bytes=64)
-        v_codes = keep.tile([P, NG, N], U32, name="v_codes", align_bytes=64)
-        v_scales = keep.tile([P, NG, N], U8, name="v_scales", align_bytes=64)
+        feat_wide = [head.tile([P, J, D], BF16, name=f"feat_wide{g}") for g in range(NG)]
+        feat_grouped = [head.tile([P, J * P, J], BF16, name=f"feat_grouped{g}", align_bytes=64) for g in range(NG)]
+        ker_grouped = [head.tile([P, 2 * P, J], BF16, name=f"ker_grouped{q}", align_bytes=64) for q in range(NQ)]
+        uv_codes = keep.tile([P, NG, NQ, 2, 2 * P], U32, name="uv_codes", align_bytes=64)
+        uv_scales = keep.tile([P, NG, NQ, 2, 2 * P], U8, name="uv_scales", align_bytes=64)
         area_col = keep.tile([P, NB], F32, name="area_col")
         area_bc = keep.tile([P, N], F32, name="area_bc")
         gate = keep.tile([P, NB, N], F32, name="gate")
 
         banks = {}
 
-        def words_in(key, slots, tag):
-            bank = psum.tile([P, 2, 2 * P], F32, name="turned", tag=tag)
+        def words_in(key, slots):
+            bank = psum.tile([P, 2, 2 * P], F32, name="turned", tag="bank_l", bufs=LAG["NL"])
             banks[key] = bank
             for s, x in enumerate(slots):
                 words = x.bitcast(F32)
@@ -118,7 +124,7 @@ def tile_dynamickernelmasksoftnms_kernel(tc, ker, feat_bytes, feat_scale, bias, 
 
         def FT(g, half):
             w = feat_wide[g]
-            words_in(("f", g, half), [w[:, 2 * half, :], w[:, 2 * half + 1, :]], "bank_l")
+            words_in(("f", g, half), [w[:, 2 * half, :], w[:, 2 * half + 1, :]])
 
         def FC(g, half):
             first = 2 * half * P
@@ -134,7 +140,7 @@ def tile_dynamickernelmasksoftnms_kernel(tc, ker, feat_bytes, feat_scale, bias, 
             nc.vector.quantize_mx(out=feat_codes[:, s].bitcast(FP8X4), scales=feat_scales[:, s], in_=feat_grouped[g][:].rearrange("p n j -> p (n j)"))
 
         def KT(q):
-            words_in(("k", q), [ker_raw[q][:, 0, :], ker_raw[q][:, 1, :]], "bank_l")
+            words_in(("k", q), [ker_raw[q][:, 0, :], ker_raw[q][:, 1, :]])
 
         def KC(q):
             dst = ker_grouped[q][:].rearrange("p n j -> p (n j)").bitcast(F32)
@@ -145,15 +151,18 @@ def tile_dynamickernelmasksoftnms_kernel(tc, ker, feat_bytes, feat_scale, bias, 
             nc.vector.quantize_mx(out=ker_codes[:, s].bitcast(FP8X4), scales=ker_scales[:, s], in_=ker_grouped[q][:].rearrange("p n j -> p (n j)"))
 
         units = [(b, g) for g in range(NG) for b in range(2)] + [(b, g) for b in range(2, NB) for g in range(NG)]
-        area_order = [(b, g) for b in range(NB) for g in range(NG)]
+        area_order = [(b, g) for b in range(NB) for g in range(NG) if b not in DT]
+        av_order = [(b, g) for b in DT for g in range(NG)]
+        na = len(area_order)
+        area_acc3 = {b: keep.tile([P, NG], F32, name=f"area_acc3_{b}") for b in DT}
         unit_of = {bg: k for k, bg in enumerate(units)}
         nu = len(units)
-        logits, ts, turned, t2s, us, vs, area_ps, spread_ps = {}, {}, {}, {}, {}, {}, {}, {}
+        logits, ts, turned, t2s, uvs, area_ps, spread_ps = {}, {}, {}, {}, {}, {}, {}
 
         def L(k):
             b, g = units[k]
             n, px = slice(b * P, (b + 1) * P), slice(g * 512, (g + 1) * 512)
-            x = psum.tile([P, D], F32, name="logits", tag="bank_l")
+            x = psum.tile([P, D], F32, name="logits", tag="bank_l", bufs=LAG["NL"])
             logits[k] = x
             nc.tensor.matmul_mx(
                 out=x[:],
@@ -172,68 +181,74 @@ def tile_dynamickernelmasksoftnms_kernel(tc, ker, feat_bytes, feat_scale, bias, 
             nc.scalar.activation(out=t[:], in_=logits[k][:], func=ACT.Tanh, bias=cols[:, b : b + 1], scale=D**-0.5)
 
         def TR(k):
-            x = psum.tile([P, J, P], F32, name="t_turned", tag="bank_t")
+            x = psum.tile([P, J, P], F32, name="t_turned", tag="bank_t", bufs=LAG["NT"])
             turned[k] = x
             for j in range(J):
                 nc.tensor.transpose(x[:, j, :], ts[k][:, j * P : (j + 1) * P], ident[:])
 
-        def gain(k, gains, store, name):
+        def UV(k):
             b, g = units[k]
             half = b % 2
             if half == 0:
-                w = work.tile([P, 2 * P, J], BF16, name=name, bufs=5, align_bytes=64)
-                store[b // 2, g] = w
+                w = work.tile([P, 2, 2 * P, J], BF16, name="uv", bufs=5, align_bytes=64)
+                uvs[b // 2, g] = w
+            shape = [P, 2, P, J]
             nc.vector.tensor_tensor(
-                out=store[b // 2, g][:, half * P : (half + 1) * P, :],
-                in0=turned[k][:].rearrange("p j n -> p n j"),
-                in1=gains[:, g, :].unsqueeze(1).to_broadcast([P, P, J]),
+                out=uvs[b // 2, g][:, :, half * P : (half + 1) * P, :],
+                in0=turned[k][:].rearrange("p j n -> p n j").unsqueeze(1).to_broadcast(shape),
+                in1=gains[:, :, g, :].unsqueeze(2).to_broadcast(shape),
                 op=ALU.mult,
             )
 
-        def quant(k, codes, scales, store):
+        def Q(k):
             b, g = units[k]
             if b % 2 == 0:
                 return
-            s = slice((b - 1) * P, (b + 1) * P)
-            nc.vector.quantize_mx(out=codes[:, g, s].bitcast(FP8X4), scales=scales[:, g, s], in_=store[b // 2, g][:].rearrange("p n j -> p (n j)"))
-
-        def U(k):
-            gain(k, gains_a, us, "u")
-
-        def V(k):
-            gain(k, gains_b, vs, "v")
-
-        def UQ(k):
-            quant(k, u_codes, u_scales, us)
-
-        def VQ(k):
-            quant(k, v_codes, v_scales, vs)
+            q = b // 2
+            nc.vector.quantize_mx(
+                out=uv_codes[:, g, q, :, :].rearrange("p s n -> p (s n)").bitcast(FP8X4),
+                scales=uv_scales[:, g, q, :, :].rearrange("p s n -> p (s n)"),
+                in_=uvs[q, g][:].rearrange("p s n j -> p (s n j)"),
+            )
 
         def S(k):
-            t2 = work.tile([P, J, P], F32, name="t2", bufs=8)
+            t2 = work.tile([P, J, P], F32, name="t2", bufs=LAG["T2"])
             t2s[k] = t2
-            nc.scalar.activation(out=t2[:], in_=turned[k][:], func=ACT.Square)
+            b, g = units[k]
+            src = ts[k][:].rearrange("p (j m) -> p j m", j=J) if b in DT else turned[k][:]
+            nc.scalar.activation(out=t2[:], in_=src, func=ACT.Square)
 
-        def AR(n):
-            b, g = area_order[n]
-            if b % 2 == 0 and g == 0:
+        def AV(n):
+            b, g = av_order[n]
+            junk = work.tile([P, J, P], F32, name="junk", bufs=1)
+            nc.vector.scalar_tensor_tensor(out=junk[:], in0=t2s[unit_of[b, g]][:], scalar=1.0, in1=gab_bc[:, g, :, :], op0=ALU.mult, op1=ALU.mult, accum_out=area_acc3[b][:, g : g + 1])
+            if g == NG - 1:
+                nc.vector.tensor_reduce(out=area_col[:, b : b + 1], in_=area_acc3[b][:], axis=mybir.AxisListType.X, op=ALU.add)
+
+        def AR(m):
+            b, g = area_order[m // J]
+            j = m % J
+            if b // 2 not in area_ps:
                 acc = psum_area.tile([P, 2, GAIN_N], F32, name="area_acc", tag="area_acc")
                 area_ps[b // 2] = acc
-            for j in range(J):
+            if True:
                 nc.tensor.matmul(
                     out=area_ps[b // 2][:, b % 2, :],
                     lhsT=t2s[unit_of[b, g]][:, j, :],
-                    rhs=gab[:, g, j : j + 1].to_broadcast([P, GAIN_N]),
+                    rhs=gab[:, g, j, :],
                     start=(g == 0 and j == 0),
                     stop=(g == NG - 1 and j == J - 1),
                 )
 
         def AO(q):
-            nc.vector.tensor_copy(out=area_col[:, 2 * q : 2 * q + 2], in_=area_ps[q][:, :, 0])
+            hs = [h for h in range(2) if 2 * q + h not in DT]
+            nc.vector.tensor_copy(out=area_col[:, 2 * q + hs[0] : 2 * q + hs[-1] + 1], in_=area_ps[q][:, hs[0] : hs[-1] + 1, 0])
 
         def SP(q):
-            pool, tag = (psum, "bank_l") if q < 2 else (psum_area, "area_acc")
-            bank = pool.tile([P, 2, P], F32, name="spread", tag=tag)
+            if q < 2:
+                bank = psum.tile([P, 2, P], F32, name="spread", tag="bank_l", bufs=LAG["NL"])
+            else:
+                bank = psum_area.tile([P, 2, P], F32, name="spread", tag="area_acc")
             spread_ps[q] = bank
             for h in range(2):
                 b = 2 * q + h
@@ -250,7 +265,7 @@ def tile_dynamickernelmasksoftnms_kernel(tc, ker, feat_bytes, feat_scale, bias, 
             nc.scalar.activation(out=gate[:, i, h * 512 : (h + 1) * 512], in_=score_bc[:, h * 512 : (h + 1) * 512], func=ACT.Sigmoid, bias=score8[:, i : i + 1], scale=-8.0)
 
         def COLS():
-            cols_ps = psum.tile([P, P], BF16, name="cols_ps", tag="bank_t")
+            cols_ps = psum.tile([P, P], BF16, name="cols_ps", tag="bank_t", bufs=LAG["NT"])
             nc.tensor.transpose(cols_ps[:], rows[:], ident_bf[:])
             nc.scalar.copy(out=cols[:], in_=cols_ps[:, 0 : 2 * NB])
             nc.scalar.activation(out=score8[:], in_=cols_ps[:, NB : 2 * NB], func=ACT.Copy, scale=8.0)
@@ -265,8 +280,17 @@ def tile_dynamickernelmasksoftnms_kernel(tc, ker, feat_bytes, feat_scale, bias, 
         def SBC(h):
             copy(SBC_ENG[h], score_bc[:, h * 512 : (h + 1) * 512], banks["s", h][:].rearrange("p b n -> p (b n)"))
 
+        def DM():
+            bank = psum.tile([P, 512], F32, name="dummy", tag="bank_t", bufs=LAG["NT"])
+            nc.tensor.matmul(out=bank[:], lhsT=zero[:, 0:P], rhs=zero[:], start=True, stop=True)
+
         def GAB():
-            nc.vector.tensor_tensor(out=gab[:], in0=gains_a[:], in1=gains_b[:], op=ALU.mult)
+            a, b = [v.unsqueeze(3).to_broadcast([P, NG, J, GAIN_N]) for v in (gains[:, 0, 0:NG, :], gains[:, 1, 0:NG, :])]
+            nc.vector.tensor_tensor(out=gab[:], in0=a, in1=b, op=ALU.mult)
+
+        def GBC(g):
+            a, b = [v[:, g, :, :].rearrange("p m j -> p j m") for v in gains_row]
+            nc.gpsimd.tensor_tensor(out=gab_bc[:, g, :, :], in0=a, in1=b, op=ALU.mult)
 
         halves = [(i, h) for h in range(2) for i in range(NB)]
         nh = len(halves)
@@ -274,18 +298,22 @@ def tile_dynamickernelmasksoftnms_kernel(tc, ker, feat_bytes, feat_scale, bias, 
 
         def X(k):
             i, h = halves[k]
-            x = psum.tile([P, 512], F32, name="x", tag=("bank_l", "bank_t")[k % 2])
+            n_l = LAG["NL"]
+            tag = "bank_l" if k % 6 < n_l else "bank_t"
+            x = psum.tile([P, 512], F32, name="x", tag=tag, bufs=n_l if tag == "bank_l" else LAG["NT"])
             xs[k] = x
-            for g in range(NG):
-                nc.tensor.matmul_mx(
-                    out=x[:],
-                    lhsT=u_codes[:, g, i * P : (i + 1) * P].bitcast(FP8X4),
-                    lhsT_scale=u_scales[:, g, i * P : (i + 1) * P],
-                    rhs=v_codes[:, g, h * 512 : (h + 1) * 512].bitcast(FP8X4),
-                    rhs_scale=v_scales[:, g, h * 512 : (h + 1) * 512],
-                    start=(g == 0),
-                    stop=(g == NG - 1),
-                )
+            qi, n = i // 2, slice((i % 2) * P, (i % 2 + 1) * P)
+            for c in range(2):
+                for g in range(NG):
+                    nc.tensor.matmul_mx(
+                        out=x[:, c * 256 : (c + 1) * 256],
+                        lhsT=uv_codes[:, g, qi, 0, n].bitcast(FP8X4),
+                        lhsT_scale=uv_scales[:, g, qi, 0, n],
+                        rhs=uv_codes[:, g, 2 * h + c, 1, :].bitcast(FP8X4),
+                        rhs_scale=uv_scales[:, g, 2 * h + c, 1, :],
+                        start=(g == 0),
+                        stop=(g == NG - 1),
+                    )
 
         def M(k):
             i, h = halves[k]
@@ -347,7 +375,7 @@ def tile_dynamickernelmasksoftnms_kernel(tc, ker, feat_bytes, feat_scale, bias, 
             eng.tensor_tensor(out=o[:], in0=es[k][:], in1=score_bc[:, s], op=ALU.mult)
             nc.sync.dma_start(out=out[i * P : (i + 1) * P, s], in_=o[:])
 
-        calls = {"W": W, "FT": FT, "FC": FC, "FQ": FQ, "KT": KT, "KC": KC, "KQ": KQ, "L": L, "TH": TH, "TR": TR, "U": U, "V": V, "UQ": UQ, "VQ": VQ, "S": S, "AR": AR, "G": G, "COLS": COLS, "GAB": GAB, "SB": SB, "SBC": SBC}
+        calls = {"W": W, "FT": FT, "FC": FC, "FQ": FQ, "KT": KT, "KC": KC, "KQ": KQ, "L": L, "TH": TH, "TR": TR, "U": UV, "Q": Q, "S": S, "AR": AR, "G": G, "DM": DM, "COLS": COLS, "GAB": GAB, "SB": SB, "SBC": SBC}
         done = {}
         for item in HEAD.split():
             name, *args = item.split(".")
@@ -365,20 +393,27 @@ def tile_dynamickernelmasksoftnms_kernel(tc, ker, feat_bytes, feat_scale, bias, 
         for k in range(first, nu + 1):
             for item in LAG["order"]:
                 if item == "L":
-                    upto(L, "L", k + LAG["L"], nu)
+                    if k % LAG["LG"] == LAG["LP"]:
+                        upto(L, "L", k + LAG["L"] + LAG["LG"] - 1, nu)
                 elif item == "TH":
                     upto(TH, "TH", k + LAG["TH"], nu)
                 elif item == "TR":
-                    upto(TR, "TR", k + LAG["TR"], nu)
+                    if k % LAG["TRG"] == LAG["TRP"]:
+                        upto(TR, "TR", k + LAG["TR"] + LAG["TRG"] - 1, nu)
                 elif item == "S":
                     upto(S, "S", k + LAG["S"], nu)
                 elif item == "AR":
-                    upto(AR, "AR", k - LAG["AR"], nu)
+                    upto(AR, "AR", int((k - LAG["AR"] + 1) * LAG["ARR"]) - 1, J * na)
+                elif item == "AV":
+                    for n, at in enumerate(LAG["AV"]):
+                        if at == k:
+                            AV(n)
+                elif item == "GBC" and k in LAG["GBC"]:
+                    GBC(LAG["GBC"].index(k))
                 elif item == "U":
-                    upto(U, "U", k, nu)
-                    upto(UQ, "UQ", k - 1, nu)
-                    upto(V, "V", k, nu)
-                    upto(VQ, "VQ", k - 1, nu)
+                    upto(UV, "U", k, nu)
+                elif item == "Q":
+                    upto(Q, "Q", k - LAG["Q"], nu)
                 elif item == "KT" and k in LAG["KT"]:
                     KT(LAG["KT"].index(k) + 2)
                 elif item == "KC" and k in LAG["KC"]:
@@ -397,10 +432,10 @@ def tile_dynamickernelmasksoftnms_kernel(tc, ker, feat_bytes, feat_scale, bias, 
                     upto(X, "X", k - nu + LAG["X"], nh)
                 elif item == "M":
                     upto(M, "M", k - nu + LAG["M"], nh)
+        upto(Q, "Q", nu, nu)
         upto(G, "G", 2 * NB - 1, 2 * NB)
         for k in range(-1, nh + 4):
-            if k <= LAG["AR"] - 2:
-                upto(AR, "AR", nu - LAG["AR"] + k + 1, nu)
+            upto(AR, "AR", max(done["AR"], int((nu + k + 2 - LAG["AR"]) * LAG["ARR"]) - 1), J * na)
             upto(X, "X", k + LAG["XA"], nh)
             upto(M, "M", k + LAG["MA"], nh)
             for q, at in LAG["late"]:

@@ -3,12 +3,7 @@ from contextlib import ExitStack
 import concourse.mybir as mybir
 from concourse.masks import make_identity
 
-N, D, PX = 1024, 512, 1536
-P = 128
-J = 4
-NB = N // P
-NG = PX // (P * J)
-NQ = NB // 2
+KERNELS, DEPTH, PIXELS = 1024, 512, 1536
 
 F32 = mybir.dt.float32
 BF16 = mybir.dt.bfloat16
@@ -19,153 +14,177 @@ FP8X4 = mybir.dt.float8_e4m3fn_x4
 ACT = mybir.ActivationFunctionType
 ALU = mybir.AluOpType
 
-FLOPS = 2 * N * PX * D + 2 * N * N * PX
-GAIN_N = 48
-HEAD = "W.2.2 DM W.0.1 W.0.3 DM DM DM W.0.0 W.0.2 FT.0.0 DM DM FT.0.1 KT.0 FC.0.0 FC.0.1 KC.0 W.1.1 GAB W.1.3 W.1.2 W.2.1 KQ.0 W.1.0 SB.0 COLS DM FT.1.0 DM DM SB.1 SBC.0 W.2.3 W.2.0 FT.1.1 FQ.0 L.0 L.1 SBC.1 FC.1.0 DM TH.0 FC.1.1 FQ.1 G.1 TH.1 FT.2.1 G.0 Q.0 TR.0 FT.2.0 TR.1 S.0 L.2 FC.2.1 L.3 FC.2.0 U.0 DM G.3 TH.2 S.1 TH.3 G.2 DM FQ.2 KT.1 KC.1 DM U.1 TR.2 KQ.1 S.2 Q.1"
-LAG = {"order": ('L', 'M', 'Q', 'AR', 'KC', 'TH', 'KQ', 'TR', 'S', 'X', 'U', 'SP', 'G', 'KT', 'AO', 'SC'), "L": 4, "TH": 3, "TR": 2, "S": 1, "AR": 2, "KT": (3, 4), "KC": (5, 9), "KQ": (7, 10), "AO": (12, 17), "SP": (15, 18), "SC": (21, 19), "G": lambda k: k >= 8 and k % 3 != 0, "X": 4, "XA": 2, "defer": 16, "OL": 0, "late": ((2, 3), (3, 4)), "M": 2, "MA": 1, "R": 1, "Y": 2, "Y2": 3, "GM": 4, "LG": 1, "LP": 0, "TRG": 2, "TRP": 0, "NL": 3, "NT": 3, "AB": 2, "ARR": 4, "T2": 8, "AV": (), "GBC": (), "Q": 2}
-D2_ENG = "apapaaapapaaaaaa"
-Y2_ENG = "daaaaaaapapaaaad"
-GM_ENG = "pppdppdppppdpddd"
-SJ_ENG = "dddddddddddddddd"
-CAST_ENG = "dpdppppdaaaa"
-KC_ENG = "aaad"
-SC_ENG = "addd"
-SBC_ENG = "aa"
-DT = ()
+FLOPS = 2 * KERNELS * PIXELS * DEPTH + 2 * KERNELS * KERNELS * PIXELS
+
+P = 128
+PACK = 4
+GROUP = P * PACK
+GROUPS = PIXELS // GROUP
+TILES = KERNELS // P
+PAIRS = TILES // 2
+HALF = KERNELS // 2
+AREA_COLS = 32
+
+UNITS = [(b, g) for g in range(GROUPS) for b in range(2)] + [(b, g) for b in range(2, TILES) for g in range(GROUPS)]
+UNIT_OF = {unit: k for k, unit in enumerate(UNITS)}
+BLOCKS = [(i, h) for h in range(2) for i in range(TILES)]
 
 
 def tile_dynamickernelmasksoftnms_kernel(tc, ker, feat_bytes, feat_scale, bias, ga, gb, score, out):
     nc = tc.nc
     with ExitStack() as ctx:
         keep = ctx.enter_context(tc.tile_pool(name="keep", bufs=1))
-        head = ctx.enter_context(tc.tile_pool(name="head", bufs=1))
         work = ctx.enter_context(tc.tile_pool(name="work", bufs=3))
-        psum = ctx.enter_context(tc.psum_pool(name="psum", bufs=3))
-        psum_area = ctx.enter_context(tc.psum_pool(name="psum_area", bufs=LAG["AB"]))
+        logit_banks = ctx.enter_context(tc.psum_pool(name="logit_banks", bufs=3))
+        mask_banks = ctx.enter_context(tc.psum_pool(name="mask_banks", bufs=3))
+        area_banks = ctx.enter_context(tc.psum_pool(name="area_banks", bufs=2))
         ctx.enter_context(tc.manual_schedule())
 
-        feat_raw = [head.tile([P, J, D], U8, name=f"feat_raw{g}") for g in range(NG)]
-        ker_raw = [head.tile([P, 2, D], BF16, name=f"ker_raw{q}") for q in range(NQ)]
+        feat_raw = [keep.tile([P, PACK, DEPTH], U8, name=f"feat_raw{g}") for g in range(GROUPS)]
+        ker_raw = [keep.tile([P, 2, DEPTH], BF16, name=f"ker_raw{q}") for q in range(PAIRS)]
 
         def load_feat(g):
-            nc.sync.dma_start(out=feat_raw[g][:], in_=feat_bytes[g * 512 : (g + 1) * 512, :].rearrange("(m j) k -> m j k", j=J))
+            rows = feat_bytes[g * GROUP : (g + 1) * GROUP, :]
+            nc.sync.dma_start(out=feat_raw[g][:], in_=rows.rearrange("(m j) k -> m j k", j=PACK))
 
         def load_ker(q):
-            nc.sync.dma_start(out=ker_raw[q][:], in_=ker[q * 256 : (q + 1) * 256, :].rearrange("(b p) k -> p b k", p=P))
+            rows = ker[q * 2 * P : (q + 1) * 2 * P, :]
+            nc.sync.dma_start(out=ker_raw[q][:], in_=rows.rearrange("(b p) k -> p b k", p=P))
 
+        feat_scale4 = keep.tile([P, PACK], F32, name="feat_scale4")
+        nc.scalar.dma_start(out=feat_scale4[:], in_=feat_scale.rearrange("o (p t) -> p (o t)", p=P, t=PACK))
         load_feat(0)
         load_ker(0)
-        rows = keep.tile([P, P], BF16, name="rows")
-        nc.vector.memset(rows[:], 0.0)
-        nc.scalar.dma_start(out=rows[0:NB, :], in_=bias.rearrange("(b p) -> b p", p=P))
-        nc.scalar.dma_start(out=rows[NB : 2 * NB, :], in_=score.rearrange("(b p) -> b p", p=P))
-        score_bc = keep.tile([P, N], F32, name="score_bc")
-        scale4 = keep.tile([P, J], F32, name="scale4")
-        nc.scalar.dma_start(out=scale4[:], in_=feat_scale.rearrange("o (p t) -> p (o t)", p=P, t=J))
+        vectors = keep.tile([P, P], BF16, name="vectors")
+        nc.vector.memset(vectors[:], 0.0)
+        nc.scalar.dma_start(out=vectors[0:TILES, :], in_=bias.rearrange("(b p) -> b p", p=P))
+        nc.scalar.dma_start(out=vectors[TILES : 2 * TILES, :], in_=score.rearrange("(b p) -> b p", p=P))
         load_feat(1)
         load_feat(2)
-        zero = keep.tile([P, 512], BF16, name="zero")
-        nc.vector.memset(zero[:], 0.0)
-        warm = keep.tile([P, 1], F32, name="warm")
-        nc.vector.memset(warm[:], 0.0)
+        gains = keep.tile([P, 2, GROUPS + 1, PACK], BF16, name="gains")
+        for i, vector in enumerate((ga, gb)):
+            nc.sync.dma_start(out=gains[:, i, 0:GROUPS, :], in_=vector.rearrange("(g m j) -> m g j", m=P, j=PACK))
+        for q in range(1, PAIRS):
+            load_ker(q)
+
         ident = keep.tile([P, P], F32, name="ident")
         make_identity(nc, ident[:])
         ident_bf = keep.tile([P, P], BF16, name="ident_bf")
         nc.gpsimd.tensor_copy(out=ident_bf[:], in_=ident[:])
-        nc.scalar.activation(out=warm[:], in_=warm[:], func=ACT.Sigmoid)
-        gains = keep.tile([P, 2, 4, J], BF16, name="gains")
-        for i, v in enumerate((ga, gb)):
-            nc.sync.dma_start(out=gains[:, i, 0:NG, :], in_=v.rearrange("(g m j) -> m g j", m=P, j=J))
-        for q in range(1, NQ):
-            load_ker(q)
+        table = keep.tile([P, 1], F32, name="table")
+        nc.vector.memset(table[:], 0.0)
+        nc.scalar.activation(out=table[:], in_=table[:], func=ACT.Sigmoid)
 
-        gab = keep.tile([P, NG, J, GAIN_N], F32, name="gab")
-        if DT:
-            gains_row = [head.tile([P, NG, P, J], BF16, name=f"gains_row{i}") for i in range(2)]
-            gab_bc = keep.tile([P, NG, J, P], F32, name="gab_bc")
-            for i, v in enumerate((ga, gb)):
-                nc.sync.dma_start(out=gains_row[i][:].rearrange("p g m j -> p (g m j)"), in_=v.partition_broadcast(P))
-        cols = keep.tile([P, 2 * NB], F32, name="cols")
-        score8 = keep.tile([P, NB], F32, name="score8")
-        feat_codes = keep.tile([P, PX], U32, name="feat_codes", align_bytes=64)
-        feat_scales = keep.tile([P, PX], U8, name="feat_scales", align_bytes=64)
-        ker_codes = keep.tile([P, N], U32, name="ker_codes", align_bytes=64)
-        ker_scales = keep.tile([P, N], U8, name="ker_scales", align_bytes=64)
-        feat_wide = [head.tile([P, J, D], BF16, name=f"feat_wide{g}") for g in range(NG)]
-        feat_grouped = [head.tile([P, J * P, J], BF16, name=f"feat_grouped{g}", align_bytes=64) for g in range(NG)]
-        ker_grouped = [head.tile([P, 2 * P, J], BF16, name=f"ker_grouped{q}", align_bytes=64) for q in range(NQ)]
-        uv_codes = keep.tile([P, NG, NQ, 2, 2 * P], U32, name="uv_codes", align_bytes=64)
-        uv_scales = keep.tile([P, NG, NQ, 2, 2 * P], U8, name="uv_scales", align_bytes=64)
-        area_col = keep.tile([P, NB], F32, name="area_col")
-        area_bc = keep.tile([P, N], F32, name="area_bc")
-        gate = keep.tile([P, NB, N], F32, name="gate")
+        bias_col = keep.tile([P, TILES], F32, name="bias_col")
+        score8_col = keep.tile([P, TILES], F32, name="score8_col")
+        score_row = keep.tile([P, KERNELS], F32, name="score_row")
+        gain_product = keep.tile([P, GROUPS, PACK, AREA_COLS], F32, name="gain_product")
+        feat_codes = keep.tile([P, PIXELS], U32, name="feat_codes", align_bytes=64)
+        feat_scales = keep.tile([P, PIXELS], U8, name="feat_scales", align_bytes=64)
+        ker_codes = keep.tile([P, KERNELS], U32, name="ker_codes", align_bytes=64)
+        ker_scales = keep.tile([P, KERNELS], U8, name="ker_scales", align_bytes=64)
+        feat_packed = [keep.tile([P, GROUP, PACK], BF16, name=f"feat_packed{g}", align_bytes=64) for g in range(GROUPS)]
+        ker_packed = [keep.tile([P, 2 * P, PACK], BF16, name=f"ker_packed{q}", align_bytes=64) for q in range(PAIRS)]
+        mask_codes = keep.tile([P, GROUPS, PAIRS, 2, 2 * P], U32, name="mask_codes", align_bytes=64)
+        mask_scales = keep.tile([P, GROUPS, PAIRS, 2, 2 * P], U8, name="mask_scales", align_bytes=64)
+        area_col = keep.tile([P, TILES], F32, name="area_col")
+        area_row = keep.tile([P, KERNELS], F32, name="area_row")
+        gate = keep.tile([P, TILES, KERNELS], F32, name="gate")
 
-        banks = {}
+        feat_wide, turned = {}, {}
 
-        def words_in(key, slots):
-            bank = psum.tile([P, 2, 2 * P], F32, name="turned", tag="bank_l", bufs=LAG["NL"])
-            banks[key] = bank
-            for s, x in enumerate(slots):
-                words = x.bitcast(F32)
-                for u in range(2):
-                    nc.tensor.transpose(bank[:, u, s * P : (s + 1) * P], words[:, u : D // 2 : 2], ident[:])
+        def turn(key, rows):
+            bank = logit_banks.tile([P, 2, 2 * P], F32, name="turned", tag="bank")
+            turned[key] = bank
+            for s in range(2):
+                words = rows[s].bitcast(F32)
+                for w in range(2):
+                    nc.tensor.transpose(bank[:, w, s * P : (s + 1) * P], words[:, w : DEPTH // 2 : 2], ident[:])
 
-        def copy(e, out, in_):
-            if e == "a":
-                nc.scalar.copy(out=out, in_=in_)
-            elif e == "d":
-                nc.vector.tensor_copy(out=out, in_=in_)
-            else:
-                nc.gpsimd.tensor_copy(out=out, in_=in_)
-
-        def W(g, j):
+        def cast_feat(g, j):
+            if j == 0:
+                wide = work.tile([P, PACK, DEPTH], BF16, name="feat_wide", bufs=2)
+                feat_wide[g] = wide
             src, dst = feat_raw[g][:, j, :].bitcast(FP8), feat_wide[g][:, j, :]
-            copy(CAST_ENG[g * J + j], dst, src)
+            if g < 2 and j % 2 == 0:
+                nc.vector.tensor_copy(out=dst, in_=src)
+            else:
+                nc.scalar.copy(out=dst, in_=src)
 
-        def FT(g, half):
-            w = feat_wide[g]
-            words_in(("f", g, half), [w[:, 2 * half, :], w[:, 2 * half + 1, :]])
+        def turn_feat(g, half):
+            turn(("feat", g, half), [feat_wide[g][:, 2 * half + s, :] for s in range(2)])
 
-        def FC(g, half):
-            first = 2 * half * P
+        def scale_feat(g, half):
+            cols = slice(half * 2 * P, (half + 1) * 2 * P)
             nc.vector.tensor_tensor(
-                out=feat_grouped[g][:, first : first + 2 * P, :].rearrange("p n (u e) -> p n u e", u=2),
-                in0=banks["f", g, half][:].bitcast(BF16).rearrange("p u (n e) -> p n u e", e=2),
-                in1=scale4[:].rearrange("p (u e) -> p u e", u=2).unsqueeze(1).to_broadcast([P, 2 * P, 2, 2]),
+                out=feat_packed[g][:, cols, :].rearrange("p n (w e) -> p n w e", w=2),
+                in0=turned["feat", g, half][:].bitcast(BF16).rearrange("p w (n e) -> p n w e", e=2),
+                in1=feat_scale4[:].rearrange("p (w e) -> p w e", w=2).unsqueeze(1).to_broadcast([P, 2 * P, 2, 2]),
                 op=ALU.mult,
             )
 
-        def FQ(g):
-            s = slice(g * 512, (g + 1) * 512)
-            nc.vector.quantize_mx(out=feat_codes[:, s].bitcast(FP8X4), scales=feat_scales[:, s], in_=feat_grouped[g][:].rearrange("p n j -> p (n j)"))
+        def quantise_feat(g):
+            cols = slice(g * GROUP, (g + 1) * GROUP)
+            nc.vector.quantize_mx(
+                out=feat_codes[:, cols].bitcast(FP8X4),
+                scales=feat_scales[:, cols],
+                in_=feat_packed[g][:].rearrange("p n t -> p (n t)"),
+            )
 
-        def KT(q):
-            words_in(("k", q), [ker_raw[q][:, 0, :], ker_raw[q][:, 1, :]])
+        def turn_ker(q):
+            turn(("ker", q), [ker_raw[q][:, s, :] for s in range(2)])
 
-        def KC(q):
-            dst = ker_grouped[q][:].rearrange("p n j -> p (n j)").bitcast(F32)
-            copy(KC_ENG[q], dst.rearrange("p (r u) -> p r u", u=2), banks["k", q][:].rearrange("p u r -> p r u"))
+        def copy_ker(q):
+            words = ker_packed[q][:].rearrange("p n t -> p (n t)").bitcast(F32)
+            nc.scalar.copy(out=words.rearrange("p (n w) -> p n w", w=2), in_=turned["ker", q][:].rearrange("p w n -> p n w"))
 
-        def KQ(q):
-            s = slice(q * 256, (q + 1) * 256)
-            nc.vector.quantize_mx(out=ker_codes[:, s].bitcast(FP8X4), scales=ker_scales[:, s], in_=ker_grouped[q][:].rearrange("p n j -> p (n j)"))
+        def quantise_ker(q):
+            cols = slice(q * 2 * P, (q + 1) * 2 * P)
+            nc.vector.quantize_mx(
+                out=ker_codes[:, cols].bitcast(FP8X4),
+                scales=ker_scales[:, cols],
+                in_=ker_packed[q][:].rearrange("p n t -> p (n t)"),
+            )
 
-        units = [(b, g) for g in range(NG) for b in range(2)] + [(b, g) for b in range(2, NB) for g in range(NG)]
-        area_order = [(b, g) for b in range(NB) for g in range(NG) if b not in DT]
-        av_order = [(b, g) for b in DT for g in range(NG)]
-        na = len(area_order)
-        area_acc3 = {b: keep.tile([P, NG], F32, name=f"area_acc3_{b}") for b in DT}
-        unit_of = {bg: k for k, bg in enumerate(units)}
-        nu = len(units)
-        logits, ts, turned, t2s, uvs, area_ps, spread_ps = {}, {}, {}, {}, {}, {}, {}
+        score_banks = {}
 
-        def L(k):
-            b, g = units[k]
-            n, px = slice(b * P, (b + 1) * P), slice(g * 512, (g + 1) * 512)
-            x = psum.tile([P, D], F32, name="logits", tag="bank_l", bufs=LAG["NL"])
-            logits[k] = x
+        def spread_score(h):
+            bank = area_banks.tile([P, TILES // 2, P], F32, name="score_bank", tag="bank")
+            score_banks[h] = bank
+            for b in range(TILES // 2):
+                row = TILES + h * (TILES // 2) + b
+                pick = ident_bf[:, row : row + 1].to_broadcast([P, P])
+                nc.tensor.matmul(out=bank[:, b, :], lhsT=pick, rhs=vectors[:], start=True, stop=True)
+
+        def copy_score(h):
+            nc.scalar.copy(out=score_row[:, h * HALF : (h + 1) * HALF], in_=score_banks[h][:].rearrange("p b n -> p (b n)"))
+
+        def make_columns():
+            bank = mask_banks.tile([P, P], BF16, name="columns", tag="bank")
+            nc.tensor.transpose(bank[:], vectors[:], ident_bf[:])
+            nc.scalar.copy(out=bias_col[:], in_=bank[:, 0:TILES])
+            nc.scalar.activation(out=score8_col[:], in_=bank[:, TILES : 2 * TILES], func=ACT.Copy, scale=8.0)
+
+        def multiply_gains():
+            a, b = [gains[:, i, 0:GROUPS, :].unsqueeze(3).to_broadcast([P, GROUPS, PACK, AREA_COLS]) for i in range(2)]
+            nc.vector.tensor_tensor(out=gain_product[:], in0=a, in1=b, op=ALU.mult)
+
+        def make_gate(n):
+            i, h = n // 2, n % 2
+            cols = slice(h * HALF, (h + 1) * HALF)
+            nc.scalar.activation(
+                out=gate[:, i, cols], in_=score_row[:, cols], func=ACT.Sigmoid, bias=score8_col[:, i : i + 1], scale=-8.0
+            )
+
+        logits, mask_tiles, turned_masks, mask_pairs, squares = {}, {}, {}, {}, {}
+
+        def make_logits(k):
+            b, g = UNITS[k]
+            n, px = slice(b * P, (b + 1) * P), slice(g * GROUP, (g + 1) * GROUP)
+            bank = logit_banks.tile([P, GROUP], F32, name="logits", tag="bank")
+            logits[k] = bank
             nc.tensor.matmul_mx(
-                out=x[:],
+                out=bank[:],
                 lhsT=ker_codes[:, n].bitcast(FP8X4),
                 lhsT_scale=ker_scales[:, n],
                 rhs=feat_codes[:, px].bitcast(FP8X4),
@@ -174,292 +193,285 @@ def tile_dynamickernelmasksoftnms_kernel(tc, ker, feat_bytes, feat_scale, bias, 
                 stop=True,
             )
 
-        def TH(k):
-            b, g = units[k]
-            t = work.tile([P, D], F32, name="t", bufs=3)
-            ts[k] = t
-            nc.scalar.activation(out=t[:], in_=logits[k][:], func=ACT.Tanh, bias=cols[:, b : b + 1], scale=D**-0.5)
+        def make_mask(k):
+            b, g = UNITS[k]
+            t = work.tile([P, GROUP], F32, name="t")
+            mask_tiles[k] = t
+            nc.scalar.activation(out=t[:], in_=logits[k][:], func=ACT.Tanh, bias=bias_col[:, b : b + 1], scale=DEPTH**-0.5)
 
-        def TR(k):
-            x = psum.tile([P, J, P], F32, name="t_turned", tag="bank_t", bufs=LAG["NT"])
-            turned[k] = x
-            for j in range(J):
-                nc.tensor.transpose(x[:, j, :], ts[k][:, j * P : (j + 1) * P], ident[:])
+        def turn_mask(k):
+            bank = mask_banks.tile([P, PACK, P], F32, name="turned_mask", tag="bank")
+            turned_masks[k] = bank
+            for j in range(PACK):
+                nc.tensor.transpose(bank[:, j, :], mask_tiles[k][:, j * P : (j + 1) * P], ident[:])
 
-        def UV(k):
-            b, g = units[k]
-            half = b % 2
-            if half == 0:
-                w = work.tile([P, 2, 2 * P, J], BF16, name="uv", bufs=5, align_bytes=64)
-                uvs[b // 2, g] = w
-            shape = [P, 2, P, J]
+        def square_mask(k):
+            t2 = work.tile([P, PACK, P], F32, name="t2", bufs=6)
+            squares[k] = t2
+            nc.scalar.activation(out=t2[:], in_=turned_masks[k][:], func=ACT.Square)
+
+        def weigh_mask(k):
+            b, g = UNITS[k]
+            q, s = b // 2, b % 2
+            if s == 0:
+                uv = work.tile([P, 2, 2 * P, PACK], BF16, name="uv", bufs=5, align_bytes=64)
+                mask_pairs[q, g] = uv
+            shape = [P, 2, P, PACK]
             nc.vector.tensor_tensor(
-                out=uvs[b // 2, g][:, :, half * P : (half + 1) * P, :],
-                in0=turned[k][:].rearrange("p j n -> p n j").unsqueeze(1).to_broadcast(shape),
+                out=mask_pairs[q, g][:, :, s * P : (s + 1) * P, :],
+                in0=turned_masks[k][:].rearrange("p j n -> p n j").unsqueeze(1).to_broadcast(shape),
                 in1=gains[:, :, g, :].unsqueeze(2).to_broadcast(shape),
                 op=ALU.mult,
             )
 
-        def Q(k):
-            b, g = units[k]
-            if b % 2 == 0:
-                return
-            q = b // 2
-            nc.vector.quantize_mx(
-                out=uv_codes[:, g, q, :, :].rearrange("p s n -> p (s n)").bitcast(FP8X4),
-                scales=uv_scales[:, g, q, :, :].rearrange("p s n -> p (s n)"),
-                in_=uvs[q, g][:].rearrange("p s n j -> p (s n j)"),
-            )
-
-        def S(k):
-            t2 = work.tile([P, J, P], F32, name="t2", bufs=LAG["T2"])
-            t2s[k] = t2
-            b, g = units[k]
-            src = ts[k][:].rearrange("p (j m) -> p j m", j=J) if b in DT else turned[k][:]
-            nc.scalar.activation(out=t2[:], in_=src, func=ACT.Square)
-
-        def AV(n):
-            b, g = av_order[n]
-            junk = work.tile([P, J, P], F32, name="junk", bufs=1)
-            nc.vector.scalar_tensor_tensor(out=junk[:], in0=t2s[unit_of[b, g]][:], scalar=1.0, in1=gab_bc[:, g, :, :], op0=ALU.mult, op1=ALU.mult, accum_out=area_acc3[b][:, g : g + 1])
-            if g == NG - 1:
-                nc.vector.tensor_reduce(out=area_col[:, b : b + 1], in_=area_acc3[b][:], axis=mybir.AxisListType.X, op=ALU.add)
-
-        def AR(m):
-            b, g = area_order[m // J]
-            j = m % J
-            if b // 2 not in area_ps:
-                acc = psum_area.tile([P, 2, GAIN_N], F32, name="area_acc", tag="area_acc")
-                area_ps[b // 2] = acc
-            if True:
-                nc.tensor.matmul(
-                    out=area_ps[b // 2][:, b % 2, :],
-                    lhsT=t2s[unit_of[b, g]][:, j, :],
-                    rhs=gab[:, g, j, :],
-                    start=(g == 0 and j == 0),
-                    stop=(g == NG - 1 and j == J - 1),
+        def quantise_pair(k):
+            b, g = UNITS[k]
+            if b % 2 == 1:
+                nc.vector.quantize_mx(
+                    out=mask_codes[:, g, b // 2, :, :].rearrange("p s n -> p (s n)").bitcast(FP8X4),
+                    scales=mask_scales[:, g, b // 2, :, :].rearrange("p s n -> p (s n)"),
+                    in_=mask_pairs[b // 2, g][:].rearrange("p s n j -> p (s n j)"),
                 )
 
-        def AO(q):
-            hs = [h for h in range(2) if 2 * q + h not in DT]
-            nc.vector.tensor_copy(out=area_col[:, 2 * q + hs[0] : 2 * q + hs[-1] + 1], in_=area_ps[q][:, hs[0] : hs[-1] + 1, 0])
+        area_sums, spread_areas = {}, {}
 
-        def SP(q):
-            if q < 2:
-                bank = psum.tile([P, 2, P], F32, name="spread", tag="bank_l", bufs=LAG["NL"])
-            else:
-                bank = psum_area.tile([P, 2, P], F32, name="spread", tag="area_acc")
-            spread_ps[q] = bank
-            for h in range(2):
-                b = 2 * q + h
-                nc.tensor.matmul(out=bank[:, h, :], lhsT=area_col[:, b : b + 1].to_broadcast([P, P]), rhs=ident[:], start=True, stop=True)
+        def sum_area(n):
+            b, g = n // GROUPS, n % GROUPS
+            if b % 2 == 0 and g == 0:
+                bank = area_banks.tile([P, 2, AREA_COLS], F32, name="area_sum", tag="bank")
+                area_sums[b // 2] = bank
+            for j in range(PACK):
+                nc.tensor.matmul(
+                    out=area_sums[b // 2][:, b % 2, :],
+                    lhsT=squares[UNIT_OF[b, g]][:, j, :],
+                    rhs=gain_product[:, g, j, :],
+                    start=(g == 0 and j == 0),
+                    stop=(g == GROUPS - 1 and j == PACK - 1),
+                )
 
-        def SC(q):
-            copy(SC_ENG[q], area_bc[:, q * 256 : (q + 1) * 256], spread_ps[q][:].rearrange("p b n -> p (b n)"))
+        def read_area(q):
+            nc.vector.tensor_copy(out=area_col[:, 2 * q : 2 * q + 2], in_=area_sums[q][:, :, 0])
 
-        g_done, gm_done = set(), set()
+        def spread_area(q):
+            pool = logit_banks if q < 2 else area_banks
+            bank = pool.tile([P, 2, P], F32, name="spread", tag="bank")
+            spread_areas[q] = bank
+            for s in range(2):
+                column = area_col[:, 2 * q + s : 2 * q + s + 1].to_broadcast([P, P])
+                nc.tensor.matmul(out=bank[:, s, :], lhsT=column, rhs=ident[:], start=True, stop=True)
 
-        def G(n):
-            i, h = divmod(n, 2)
-            g_done.add(n)
-            nc.scalar.activation(out=gate[:, i, h * 512 : (h + 1) * 512], in_=score_bc[:, h * 512 : (h + 1) * 512], func=ACT.Sigmoid, bias=score8[:, i : i + 1], scale=-8.0)
+        def copy_area(q):
+            cols = slice(q * 2 * P, (q + 1) * 2 * P)
+            nc.vector.tensor_copy(out=area_row[:, cols], in_=spread_areas[q][:].rearrange("p s n -> p (s n)"))
 
-        def COLS():
-            cols_ps = psum.tile([P, P], BF16, name="cols_ps", tag="bank_t", bufs=LAG["NT"])
-            nc.tensor.transpose(cols_ps[:], rows[:], ident_bf[:])
-            nc.scalar.copy(out=cols[:], in_=cols_ps[:, 0 : 2 * NB])
-            nc.scalar.activation(out=score8[:], in_=cols_ps[:, NB : 2 * NB], func=ACT.Copy, scale=8.0)
+        overlaps, minus_x, s_squares, reciprocals, ratios, ratio_squares = {}, {}, {}, {}, {}, {}
+        s_squared_on_gpsimd = (1, 3)
 
-        def SB(h):
-            bank = psum_area.tile([P, 4, P], F32, name="score_ps", tag="area_acc")
-            banks["s", h] = bank
-            for b in range(4):
-                r = NB + 4 * h + b
-                nc.tensor.matmul(out=bank[:, b, :], lhsT=ident_bf[:, r : r + 1].to_broadcast([P, P]), rhs=rows[:], start=True, stop=True)
+        def half_of(h):
+            return slice(h * HALF, (h + 1) * HALF)
 
-        def SBC(h):
-            copy(SBC_ENG[h], score_bc[:, h * 512 : (h + 1) * 512], banks["s", h][:].rearrange("p b n -> p (b n)"))
-
-        def DM():
-            bank = psum.tile([P, 512], F32, name="dummy", tag="bank_t", bufs=LAG["NT"])
-            nc.tensor.matmul(out=bank[:], lhsT=zero[:, 0:P], rhs=zero[:], start=True, stop=True)
-
-        def GAB():
-            a, b = [v.unsqueeze(3).to_broadcast([P, NG, J, GAIN_N]) for v in (gains[:, 0, 0:NG, :], gains[:, 1, 0:NG, :])]
-            nc.vector.tensor_tensor(out=gab[:], in0=a, in1=b, op=ALU.mult)
-
-        def GBC(g):
-            a, b = [v[:, g, :, :].rearrange("p m j -> p j m") for v in gains_row]
-            nc.gpsimd.tensor_tensor(out=gab_bc[:, g, :, :], in0=a, in1=b, op=ALU.mult)
-
-        halves = [(i, h) for h in range(2) for i in range(NB)]
-        nh = len(halves)
-        xs, ms, ds, rs, ys, y2s, es = {}, {}, {}, {}, {}, {}, {}
-
-        def X(k):
-            i, h = halves[k]
-            n_l = LAG["NL"]
-            tag = "bank_l" if k % 6 < n_l else "bank_t"
-            x = psum.tile([P, 512], F32, name="x", tag=tag, bufs=n_l if tag == "bank_l" else LAG["NT"])
-            xs[k] = x
-            qi, n = i // 2, slice((i % 2) * P, (i % 2 + 1) * P)
+        def make_overlap(k):
+            i, h = BLOCKS[k]
+            pool = logit_banks if k % 6 < 3 else mask_banks
+            bank = pool.tile([P, HALF], F32, name="overlap", tag="bank")
+            overlaps[k] = bank
+            rows = slice((i % 2) * P, (i % 2 + 1) * P)
             for c in range(2):
-                for g in range(NG):
+                for g in range(GROUPS):
                     nc.tensor.matmul_mx(
-                        out=x[:, c * 256 : (c + 1) * 256],
-                        lhsT=uv_codes[:, g, qi, 0, n].bitcast(FP8X4),
-                        lhsT_scale=uv_scales[:, g, qi, 0, n],
-                        rhs=uv_codes[:, g, 2 * h + c, 1, :].bitcast(FP8X4),
-                        rhs_scale=uv_scales[:, g, 2 * h + c, 1, :],
+                        out=bank[:, c * 2 * P : (c + 1) * 2 * P],
+                        lhsT=mask_codes[:, g, i // 2, 0, rows].bitcast(FP8X4),
+                        lhsT_scale=mask_scales[:, g, i // 2, 0, rows],
+                        rhs=mask_codes[:, g, 2 * h + c, 1, :].bitcast(FP8X4),
+                        rhs_scale=mask_scales[:, g, 2 * h + c, 1, :],
                         start=(g == 0),
-                        stop=(g == NG - 1),
+                        stop=(g == GROUPS - 1),
                     )
 
-        def M(k):
-            i, h = halves[k]
-            m = work.tile([P, 512], F32, name="m", bufs=4)
-            ms[k] = m
-            if D2_ENG[k] == "a":
-                nc.vector.tensor_tensor(out=m[:], in0=area_bc[:, h * 512 : (h + 1) * 512], in1=xs[k][:], op=ALU.subtract)
+        def subtract_overlap(k):
+            i, h = BLOCKS[k]
+            d = work.tile([P, HALF], F32, name="d")
+            minus_x[k] = d
+            if k in s_squared_on_gpsimd:
+                nc.vector.scalar_tensor_tensor(
+                    out=d[:],
+                    in0=overlaps[k][:],
+                    scalar=area_col[:, i : i + 1],
+                    in1=area_row[:, half_of(h)],
+                    op0=ALU.subtract,
+                    op1=ALU.subtract,
+                )
             else:
-                nc.vector.scalar_tensor_tensor(out=m[:], in0=xs[k][:], scalar=area_col[:, i : i + 1], in1=area_bc[:, h * 512 : (h + 1) * 512], op0=ALU.subtract, op1=ALU.subtract)
+                nc.vector.tensor_tensor(out=d[:], in0=area_row[:, half_of(h)], in1=overlaps[k][:], op=ALU.subtract)
 
-        def D2(k):
-            i, h = halves[k]
-            d2 = work.tile([P, 512], F32, name="d2", bufs=4)
-            ds[k] = d2
-            if D2_ENG[k] == "a":
-                nc.scalar.activation(out=d2[:], in_=ms[k][:], func=ACT.Square, bias=area_col[:, i : i + 1])
+        def square_s(k):
+            i, h = BLOCKS[k]
+            s2 = work.tile([P, HALF], F32, name="s2")
+            s_squares[k] = s2
+            if k in s_squared_on_gpsimd:
+                nc.gpsimd.tensor_tensor(out=s2[:], in0=minus_x[k][:], in1=minus_x[k][:], op=ALU.mult)
             else:
-                nc.gpsimd.tensor_tensor(out=d2[:], in0=ms[k][:], in1=ms[k][:], op=ALU.mult)
+                nc.scalar.activation(out=s2[:], in_=minus_x[k][:], func=ACT.Square, bias=area_col[:, i : i + 1])
 
-        def R(k):
-            r = work.tile([P, 512], F32, name="r", bufs=4)
-            rs[k] = r
-            nc.scalar.activation(out=r[:], in_=ds[k][:], func=ACT.Abs_reciprocal_sqrt)
+        def invert_s(k):
+            r = work.tile([P, HALF], F32, name="r")
+            reciprocals[k] = r
+            nc.scalar.activation(out=r[:], in_=s_squares[k][:], func=ACT.Abs_reciprocal_sqrt)
 
-        def Y(k):
-            y = work.tile([P, 512], F32, name="y")
-            ys[k] = y
-            nc.vector.tensor_tensor(out=y[:], in0=xs[k][:], in1=rs[k][:], op=ALU.mult)
+        def make_ratio(k):
+            y = work.tile([P, HALF], F32, name="y")
+            ratios[k] = y
+            nc.vector.tensor_tensor(out=y[:], in0=overlaps[k][:], in1=reciprocals[k][:], op=ALU.mult)
 
-        def Y2(k):
-            y2 = work.tile([P, 512], F32, name="y2")
-            y2s[k] = y2
-            if Y2_ENG[k] == "a":
-                nc.scalar.activation(out=y2[:], in_=ys[k][:], func=ACT.Square)
+        def square_ratio(k):
+            y2 = work.tile([P, HALF], F32, name="y2")
+            ratio_squares[k] = y2
+            if k % 3 == 0 and k > 0:
+                nc.vector.tensor_tensor(out=y2[:], in0=ratios[k][:], in1=ratios[k][:], op=ALU.mult)
             else:
-                eng = nc.vector if Y2_ENG[k] == "d" else nc.gpsimd
-                eng.tensor_tensor(out=y2[:], in0=ys[k][:], in1=ys[k][:], op=ALU.mult)
+                nc.scalar.activation(out=y2[:], in_=ratios[k][:], func=ACT.Square)
 
-        def GM(k):
-            i, h = halves[k]
-            s = slice(h * 512, (h + 1) * 512)
-            eng = nc.gpsimd if GM_ENG[k] == "p" else nc.vector
-            assert g_done >= {2 * i + h}
-            gm_done.add(k)
-            eng.tensor_tensor(out=gate[:, i, s], in0=y2s[k][:], in1=gate[:, i, s], op=ALU.mult)
+        def apply_gate(k):
+            i, h = BLOCKS[k]
+            engine = nc.gpsimd if k < 12 else nc.vector
+            engine.tensor_tensor(
+                out=gate[:, i, half_of(h)], in0=ratio_squares[k][:], in1=gate[:, i, half_of(h)], op=ALU.mult
+            )
 
-        def E(k):
-            i, h = halves[k]
-            assert k in gm_done
-            e = work.tile([P, 512], F32, name="e", bufs=4)
-            es[k] = e
-            nc.scalar.activation(out=e[:], in_=gate[:, i, h * 512 : (h + 1) * 512], func=ACT.Exp, scale=-256.0)
+        def decay(i, h):
+            e = work.tile([P, HALF], F32, name="e", bufs=4)
+            nc.scalar.activation(out=e[:], in_=gate[:, i, half_of(h)], func=ACT.Exp, scale=-256.0)
+            o = work.tile([P, HALF], F32, name="o", bufs=6)
+            nc.vector.tensor_tensor(out=o[:], in0=e[:], in1=score_row[:, half_of(h)], op=ALU.mult)
+            nc.sync.dma_start(out=out[i * P : (i + 1) * P, half_of(h)], in_=o[:])
 
-        def O(k):
-            i, h = halves[k]
-            s = slice(h * 512, (h + 1) * 512)
-            o = work.tile([P, 512], F32, name="o", bufs=6)
-            eng = nc.gpsimd if SJ_ENG[k] == "p" else nc.vector
-            eng.tensor_tensor(out=o[:], in0=es[k][:], in1=score_bc[:, s], op=ALU.mult)
-            nc.sync.dma_start(out=out[i * P : (i + 1) * P, s], in_=o[:])
+        cast_feat(0, 0)
+        cast_feat(0, 1)
+        cast_feat(0, 2)
+        cast_feat(0, 3)
+        turn_ker(0)
+        cast_feat(1, 0)
+        cast_feat(1, 1)
+        turn_feat(0, 0)
+        copy_ker(0)
+        cast_feat(1, 2)
+        multiply_gains()
+        cast_feat(1, 3)
+        turn_feat(0, 1)
+        cast_feat(2, 0)
+        make_columns()
+        cast_feat(2, 1)
+        spread_score(0)
+        scale_feat(0, 0)
+        scale_feat(0, 1)
+        turn_feat(1, 0)
+        spread_score(1)
+        quantise_ker(0)
+        cast_feat(2, 2)
+        copy_score(0)
+        quantise_feat(0)
+        turn_feat(1, 1)
+        copy_score(1)
+        make_gate(0)
+        scale_feat(1, 0)
+        make_logits(0)
+        make_mask(0)
+        cast_feat(2, 3)
+        make_logits(1)
+        turn_feat(2, 0)
+        scale_feat(1, 1)
+        make_gate(1)
+        make_mask(1)
+        quantise_feat(1)
+        make_gate(2)
+        turn_mask(0)
+        turn_feat(2, 1)
+        make_logits(2)
+        scale_feat(2, 0)
+        make_logits(3)
+        scale_feat(2, 1)
+        quantise_feat(2)
+        square_mask(0)
+        make_mask(2)
+        make_gate(3)
+        turn_mask(1)
+        square_mask(1)
+        turn_ker(1)
+        turn_mask(2)
+        copy_ker(1)
+        make_mask(3)
+        make_logits(4)
+        make_mask(4)
+        make_logits(5)
+        weigh_mask(0)
+        make_mask(5)
+        quantise_ker(1)
+        weigh_mask(1)
+        square_mask(2)
+        quantise_pair(1)
+        turn_mask(3)
+        units = len(UNITS)
+        for k in range(2, units + 1):
+            if k % 2 == 0 and k >= 4:
+                make_gate(2 + k // 2)
+            if k in (4, 5):
+                copy_ker(k - 2)
+            if k in (6, 7):
+                quantise_ker(k - 4)
+            if k in (3, 4):
+                turn_ker(k - 1)
+            sum_area(k - 2)
+            if k in (14, 20):
+                copy_area((k - 14) // 6)
+            if k + 4 < units:
+                make_logits(k + 4)
+            if k in (8, 14):
+                read_area((k - 8) // 6)
+            if k + 3 < units:
+                make_mask(k + 3)
+            if k in (12, 18):
+                spread_area((k - 12) // 6)
+            if k + 2 < units:
+                turn_mask(k + 2)
+            if k >= units - 4:
+                make_overlap(k - units + 4)
+            if k >= units - 2:
+                subtract_overlap(k - units + 2)
+            if k < units:
+                weigh_mask(k)
+            if k >= 6:
+                quantise_pair(k - 3)
+            if k + 1 < units:
+                square_mask(k + 1)
+        quantise_pair(units - 2)
+        quantise_pair(units - 1)
+        make_gate(2 * TILES - 1)
 
-        calls = {"W": W, "FT": FT, "FC": FC, "FQ": FQ, "KT": KT, "KC": KC, "KQ": KQ, "L": L, "TH": TH, "TR": TR, "U": UV, "Q": Q, "S": S, "AR": AR, "G": G, "DM": DM, "COLS": COLS, "GAB": GAB, "SB": SB, "SBC": SBC}
-        done = {}
-        for item in HEAD.split():
-            name, *args = item.split(".")
-            args = [int(a) for a in args]
-            calls[name](*args)
-            if len(args) == 1:
-                done[name] = max(done.get(name, -1), args[0])
-
-        def upto(fn, name, k, last):
-            while done.get(name, -1) < min(k, last - 1):
-                done[name] = done.get(name, -1) + 1
-                fn(done[name])
-
-        first = done.get("U", -1) + 1
-        for k in range(first, nu + 1):
-            for item in LAG["order"]:
-                if item == "L":
-                    if k % LAG["LG"] == LAG["LP"]:
-                        upto(L, "L", k + LAG["L"] + LAG["LG"] - 1, nu)
-                elif item == "TH":
-                    upto(TH, "TH", k + LAG["TH"], nu)
-                elif item == "TR":
-                    if k % LAG["TRG"] == LAG["TRP"]:
-                        upto(TR, "TR", k + LAG["TR"] + LAG["TRG"] - 1, nu)
-                elif item == "S":
-                    upto(S, "S", k + LAG["S"], nu)
-                elif item == "AR":
-                    upto(AR, "AR", int((k - LAG["AR"] + 1) * LAG["ARR"]) - 1, J * na)
-                elif item == "AV":
-                    for n, at in enumerate(LAG["AV"]):
-                        if at == k:
-                            AV(n)
-                elif item == "GBC" and k in LAG["GBC"]:
-                    GBC(LAG["GBC"].index(k))
-                elif item == "U":
-                    upto(UV, "U", k, nu)
-                elif item == "Q":
-                    upto(Q, "Q", k - LAG["Q"], nu)
-                elif item == "KT" and k in LAG["KT"]:
-                    KT(LAG["KT"].index(k) + 2)
-                elif item == "KC" and k in LAG["KC"]:
-                    KC(LAG["KC"].index(k) + 2)
-                elif item == "KQ" and k in LAG["KQ"]:
-                    KQ(LAG["KQ"].index(k) + 2)
-                elif item == "AO" and k in LAG["AO"]:
-                    AO(LAG["AO"].index(k))
-                elif item == "SP" and k in LAG["SP"]:
-                    SP(LAG["SP"].index(k))
-                elif item == "SC" and k in LAG["SC"]:
-                    SC(LAG["SC"].index(k))
-                elif item == "G" and LAG["G"](k):
-                    upto(G, "G", done["G"] + 1, 2 * NB)
-                elif item == "X":
-                    upto(X, "X", k - nu + LAG["X"], nh)
-                elif item == "M":
-                    upto(M, "M", k - nu + LAG["M"], nh)
-        upto(Q, "Q", nu, nu)
-        upto(G, "G", 2 * NB - 1, 2 * NB)
-        for k in range(-1, nh + 4):
-            upto(AR, "AR", max(done["AR"], int((nu + k + 2 - LAG["AR"]) * LAG["ARR"]) - 1), J * na)
-            upto(X, "X", k + LAG["XA"], nh)
-            upto(M, "M", k + LAG["MA"], nh)
-            for q, at in LAG["late"]:
-                if k == at:
-                    AO(q)
-                if k == at + 1:
-                    SP(q)
-                if k == at + 2:
-                    SC(q)
-            upto(D2, "D2", k, nh)
-            upto(R, "R", k - LAG["R"], nh)
-            upto(Y, "Y", k - LAG["Y"], nh)
-            upto(Y2, "Y2", k - LAG["Y2"], LAG["defer"])
-            upto(GM, "GM", k - LAG["GM"], LAG["defer"])
-        upto(Y, "Y", nh, nh)
-        upto(Y2, "Y2", nh, LAG["defer"])
-        upto(GM, "GM", nh, LAG["defer"])
-        nxt = LAG["defer"]
-        for k in range(nh + LAG["OL"]):
-            if k < nh:
-                E(k)
-            if nxt < nh:
-                Y2(nxt)
-                GM(nxt)
-                nxt += 1
-            if k >= LAG["OL"]:
-                O(k - LAG["OL"])
+        blocks = len(BLOCKS)
+        for k in range(blocks + 4):
+            if k == 0:
+                sum_area(units - 1)
+            if 5 <= k + 2 < blocks:
+                make_overlap(k + 2)
+            if 3 <= k + 1 < blocks:
+                subtract_overlap(k + 1)
+            for q in (2, 3):
+                if k == q + 1:
+                    read_area(q)
+                if k == q + 2:
+                    spread_area(q)
+                if k == q + 3:
+                    copy_area(q)
+            if k < blocks:
+                square_s(k)
+            if 0 <= k - 1 < blocks:
+                invert_s(k - 1)
+            if 0 <= k - 2 < blocks:
+                make_ratio(k - 2)
+            if 0 <= k - 3 < blocks:
+                square_ratio(k - 3)
+            if 0 <= k - 4 < blocks:
+                apply_gate(k - 4)
+        for i in range(TILES):
+            for h in range(2):
+                decay(i, h)

from contextlib import ExitStack

import concourse.mybir as mybir
from concourse.masks import make_identity

KERNELS, DEPTH, PIXELS = 1024, 512, 1536

F32 = mybir.dt.float32
BF16 = mybir.dt.bfloat16
U32 = mybir.dt.uint32
U8 = mybir.dt.uint8
FP8 = mybir.dt.float8_e4m3fn
FP8X4 = mybir.dt.float8_e4m3fn_x4
ACT = mybir.ActivationFunctionType
ALU = mybir.AluOpType

FLOPS = 2 * KERNELS * PIXELS * DEPTH + 2 * KERNELS * KERNELS * PIXELS

P = 128
PACK = 4
GROUP = P * PACK
GROUPS = PIXELS // GROUP
TILES = KERNELS // P
PAIRS = TILES // 2
HALF = KERNELS // 2
AREA_COLS = 32

UNITS = [(b, g) for g in range(GROUPS) for b in range(2)] + [(b, g) for b in range(2, TILES) for g in range(GROUPS)]
UNIT_OF = {unit: k for k, unit in enumerate(UNITS)}
BLOCKS = [(i, h) for h in range(2) for i in range(TILES)]


def tile_dynamickernelmasksoftnms_kernel(tc, ker, feat_bytes, feat_scale, bias, ga, gb, score, out):
    nc = tc.nc
    with ExitStack() as ctx:
        keep = ctx.enter_context(tc.tile_pool(name="keep", bufs=1))
        work = ctx.enter_context(tc.tile_pool(name="work", bufs=3))
        logit_banks = ctx.enter_context(tc.psum_pool(name="logit_banks", bufs=3))
        mask_banks = ctx.enter_context(tc.psum_pool(name="mask_banks", bufs=3))
        area_banks = ctx.enter_context(tc.psum_pool(name="area_banks", bufs=2))
        ctx.enter_context(tc.manual_schedule())

        feat_raw = [keep.tile([P, PACK, DEPTH], U8, name=f"feat_raw{g}") for g in range(GROUPS)]
        ker_raw = [keep.tile([P, 2, DEPTH], BF16, name=f"ker_raw{q}") for q in range(PAIRS)]

        def load_feat(g):
            rows = feat_bytes[g * GROUP : (g + 1) * GROUP, :]
            nc.sync.dma_start(out=feat_raw[g][:], in_=rows.rearrange("(m j) k -> m j k", j=PACK))

        def load_ker(q):
            rows = ker[q * 2 * P : (q + 1) * 2 * P, :]
            nc.sync.dma_start(out=ker_raw[q][:], in_=rows.rearrange("(b p) k -> p b k", p=P))

        feat_scale4 = keep.tile([P, PACK], F32, name="feat_scale4")
        nc.scalar.dma_start(out=feat_scale4[:], in_=feat_scale.rearrange("o (p t) -> p (o t)", p=P, t=PACK))
        load_feat(0)
        load_ker(0)
        vectors = keep.tile([P, P], BF16, name="vectors")
        nc.vector.memset(vectors[:], 0.0)
        nc.scalar.dma_start(out=vectors[0:TILES, :], in_=bias.rearrange("(b p) -> b p", p=P))
        nc.scalar.dma_start(out=vectors[TILES : 2 * TILES, :], in_=score.rearrange("(b p) -> b p", p=P))
        load_feat(1)
        load_feat(2)
        gains = keep.tile([P, 2, GROUPS + 1, PACK], BF16, name="gains")
        for i, vector in enumerate((ga, gb)):
            nc.sync.dma_start(out=gains[:, i, 0:GROUPS, :], in_=vector.rearrange("(g m j) -> m g j", m=P, j=PACK))
        for q in range(1, PAIRS):
            load_ker(q)

        ident = keep.tile([P, P], F32, name="ident")
        make_identity(nc, ident[:])
        ident_bf = keep.tile([P, P], BF16, name="ident_bf")
        nc.gpsimd.tensor_copy(out=ident_bf[:], in_=ident[:])
        table = keep.tile([P, 1], F32, name="table")
        nc.vector.memset(table[:], 0.0)
        nc.scalar.activation(out=table[:], in_=table[:], func=ACT.Sigmoid)

        bias_col = keep.tile([P, TILES], F32, name="bias_col")
        score8_col = keep.tile([P, TILES], F32, name="score8_col")
        score_row = keep.tile([P, KERNELS], F32, name="score_row")
        gain_product = keep.tile([P, GROUPS, PACK, AREA_COLS], F32, name="gain_product")
        feat_codes = keep.tile([P, PIXELS], U32, name="feat_codes", align_bytes=64)
        feat_scales = keep.tile([P, PIXELS], U8, name="feat_scales", align_bytes=64)
        ker_codes = keep.tile([P, KERNELS], U32, name="ker_codes", align_bytes=64)
        ker_scales = keep.tile([P, KERNELS], U8, name="ker_scales", align_bytes=64)
        feat_packed = [keep.tile([P, GROUP, PACK], BF16, name=f"feat_packed{g}", align_bytes=64) for g in range(GROUPS)]
        ker_packed = [keep.tile([P, 2 * P, PACK], BF16, name=f"ker_packed{q}", align_bytes=64) for q in range(PAIRS)]
        mask_codes = keep.tile([P, GROUPS, PAIRS, 2, 2 * P], U32, name="mask_codes", align_bytes=64)
        mask_scales = keep.tile([P, GROUPS, PAIRS, 2, 2 * P], U8, name="mask_scales", align_bytes=64)
        area_col = keep.tile([P, TILES], F32, name="area_col")
        area_row = keep.tile([P, KERNELS], F32, name="area_row")
        gate = keep.tile([P, TILES, KERNELS], F32, name="gate")

        feat_wide, turned = {}, {}

        def turn(key, rows):
            bank = logit_banks.tile([P, 2, 2 * P], F32, name="turned", tag="bank")
            turned[key] = bank
            for s in range(2):
                words = rows[s].bitcast(F32)
                for w in range(2):
                    nc.tensor.transpose(bank[:, w, s * P : (s + 1) * P], words[:, w : DEPTH // 2 : 2], ident[:])

        def cast_feat(g, j):
            if j == 0:
                wide = work.tile([P, PACK, DEPTH], BF16, name="feat_wide", bufs=2)
                feat_wide[g] = wide
            src, dst = feat_raw[g][:, j, :].bitcast(FP8), feat_wide[g][:, j, :]
            if g < 2 and j % 2 == 0:
                nc.vector.tensor_copy(out=dst, in_=src)
            else:
                nc.scalar.copy(out=dst, in_=src)

        def turn_feat(g, half):
            turn(("feat", g, half), [feat_wide[g][:, 2 * half + s, :] for s in range(2)])

        def scale_feat(g, half):
            cols = slice(half * 2 * P, (half + 1) * 2 * P)
            nc.vector.tensor_tensor(
                out=feat_packed[g][:, cols, :].rearrange("p n (w e) -> p n w e", w=2),
                in0=turned["feat", g, half][:].bitcast(BF16).rearrange("p w (n e) -> p n w e", e=2),
                in1=feat_scale4[:].rearrange("p (w e) -> p w e", w=2).unsqueeze(1).to_broadcast([P, 2 * P, 2, 2]),
                op=ALU.mult,
            )

        def quantise_feat(g):
            cols = slice(g * GROUP, (g + 1) * GROUP)
            nc.vector.quantize_mx(
                out=feat_codes[:, cols].bitcast(FP8X4),
                scales=feat_scales[:, cols],
                in_=feat_packed[g][:].rearrange("p n t -> p (n t)"),
            )

        def turn_ker(q):
            turn(("ker", q), [ker_raw[q][:, s, :] for s in range(2)])

        def copy_ker(q):
            words = ker_packed[q][:].rearrange("p n t -> p (n t)").bitcast(F32)
            nc.scalar.copy(out=words.rearrange("p (n w) -> p n w", w=2), in_=turned["ker", q][:].rearrange("p w n -> p n w"))

        def quantise_ker(q):
            cols = slice(q * 2 * P, (q + 1) * 2 * P)
            nc.vector.quantize_mx(
                out=ker_codes[:, cols].bitcast(FP8X4),
                scales=ker_scales[:, cols],
                in_=ker_packed[q][:].rearrange("p n t -> p (n t)"),
            )

        score_banks = {}

        def spread_score(h):
            bank = area_banks.tile([P, TILES // 2, P], F32, name="score_bank", tag="bank")
            score_banks[h] = bank
            for b in range(TILES // 2):
                row = TILES + h * (TILES // 2) + b
                pick = ident_bf[:, row : row + 1].to_broadcast([P, P])
                nc.tensor.matmul(out=bank[:, b, :], lhsT=pick, rhs=vectors[:], start=True, stop=True)

        def copy_score(h):
            nc.scalar.copy(out=score_row[:, h * HALF : (h + 1) * HALF], in_=score_banks[h][:].rearrange("p b n -> p (b n)"))

        def make_columns():
            bank = mask_banks.tile([P, P], BF16, name="columns", tag="bank")
            nc.tensor.transpose(bank[:], vectors[:], ident_bf[:])
            nc.scalar.copy(out=bias_col[:], in_=bank[:, 0:TILES])
            nc.scalar.activation(out=score8_col[:], in_=bank[:, TILES : 2 * TILES], func=ACT.Copy, scale=8.0)

        def multiply_gains():
            a, b = [gains[:, i, 0:GROUPS, :].unsqueeze(3).to_broadcast([P, GROUPS, PACK, AREA_COLS]) for i in range(2)]
            nc.vector.tensor_tensor(out=gain_product[:], in0=a, in1=b, op=ALU.mult)

        def make_gate(n):
            i, h = n // 2, n % 2
            cols = slice(h * HALF, (h + 1) * HALF)
            nc.scalar.activation(
                out=gate[:, i, cols], in_=score_row[:, cols], func=ACT.Sigmoid, bias=score8_col[:, i : i + 1], scale=-8.0
            )

        logits, mask_tiles, turned_masks, mask_pairs, squares = {}, {}, {}, {}, {}

        def make_logits(k):
            b, g = UNITS[k]
            n, px = slice(b * P, (b + 1) * P), slice(g * GROUP, (g + 1) * GROUP)
            bank = logit_banks.tile([P, GROUP], F32, name="logits", tag="bank")
            logits[k] = bank
            nc.tensor.matmul_mx(
                out=bank[:],
                lhsT=ker_codes[:, n].bitcast(FP8X4),
                lhsT_scale=ker_scales[:, n],
                rhs=feat_codes[:, px].bitcast(FP8X4),
                rhs_scale=feat_scales[:, px],
                start=True,
                stop=True,
            )

        def make_mask(k):
            b, g = UNITS[k]
            t = work.tile([P, GROUP], F32, name="t")
            mask_tiles[k] = t
            nc.scalar.activation(out=t[:], in_=logits[k][:], func=ACT.Tanh, bias=bias_col[:, b : b + 1], scale=DEPTH**-0.5)

        def turn_mask(k):
            bank = mask_banks.tile([P, PACK, P], F32, name="turned_mask", tag="bank")
            turned_masks[k] = bank
            for j in range(PACK):
                nc.tensor.transpose(bank[:, j, :], mask_tiles[k][:, j * P : (j + 1) * P], ident[:])

        def square_mask(k):
            t2 = work.tile([P, PACK, P], F32, name="t2", bufs=6)
            squares[k] = t2
            nc.scalar.activation(out=t2[:], in_=turned_masks[k][:], func=ACT.Square)

        def weigh_mask(k):
            b, g = UNITS[k]
            q, s = b // 2, b % 2
            if s == 0:
                uv = work.tile([P, 2, 2 * P, PACK], BF16, name="uv", bufs=5, align_bytes=64)
                mask_pairs[q, g] = uv
            shape = [P, 2, P, PACK]
            nc.vector.tensor_tensor(
                out=mask_pairs[q, g][:, :, s * P : (s + 1) * P, :],
                in0=turned_masks[k][:].rearrange("p j n -> p n j").unsqueeze(1).to_broadcast(shape),
                in1=gains[:, :, g, :].unsqueeze(2).to_broadcast(shape),
                op=ALU.mult,
            )

        def quantise_pair(k):
            b, g = UNITS[k]
            if b % 2 == 1:
                nc.vector.quantize_mx(
                    out=mask_codes[:, g, b // 2, :, :].rearrange("p s n -> p (s n)").bitcast(FP8X4),
                    scales=mask_scales[:, g, b // 2, :, :].rearrange("p s n -> p (s n)"),
                    in_=mask_pairs[b // 2, g][:].rearrange("p s n j -> p (s n j)"),
                )

        area_sums, spread_areas = {}, {}

        def sum_area(n):
            b, g = n // GROUPS, n % GROUPS
            if b % 2 == 0 and g == 0:
                bank = area_banks.tile([P, 2, AREA_COLS], F32, name="area_sum", tag="bank")
                area_sums[b // 2] = bank
            for j in range(PACK):
                nc.tensor.matmul(
                    out=area_sums[b // 2][:, b % 2, :],
                    lhsT=squares[UNIT_OF[b, g]][:, j, :],
                    rhs=gain_product[:, g, j, :],
                    start=(g == 0 and j == 0),
                    stop=(g == GROUPS - 1 and j == PACK - 1),
                )

        def read_area(q):
            nc.vector.tensor_copy(out=area_col[:, 2 * q : 2 * q + 2], in_=area_sums[q][:, :, 0])

        def spread_area(q):
            pool = logit_banks if q < 2 else area_banks
            bank = pool.tile([P, 2, P], F32, name="spread", tag="bank")
            spread_areas[q] = bank
            for s in range(2):
                column = area_col[:, 2 * q + s : 2 * q + s + 1].to_broadcast([P, P])
                nc.tensor.matmul(out=bank[:, s, :], lhsT=column, rhs=ident[:], start=True, stop=True)

        def copy_area(q):
            cols = slice(q * 2 * P, (q + 1) * 2 * P)
            nc.vector.tensor_copy(out=area_row[:, cols], in_=spread_areas[q][:].rearrange("p s n -> p (s n)"))

        overlaps, minus_x, s_squares, reciprocals, ratios, ratio_squares = {}, {}, {}, {}, {}, {}
        s_squared_on_gpsimd = (1, 3)

        def half_of(h):
            return slice(h * HALF, (h + 1) * HALF)

        def make_overlap(k):
            i, h = BLOCKS[k]
            pool = logit_banks if k % 6 < 3 else mask_banks
            bank = pool.tile([P, HALF], F32, name="overlap", tag="bank")
            overlaps[k] = bank
            rows = slice((i % 2) * P, (i % 2 + 1) * P)
            for c in range(2):
                for g in range(GROUPS):
                    nc.tensor.matmul_mx(
                        out=bank[:, c * 2 * P : (c + 1) * 2 * P],
                        lhsT=mask_codes[:, g, i // 2, 0, rows].bitcast(FP8X4),
                        lhsT_scale=mask_scales[:, g, i // 2, 0, rows],
                        rhs=mask_codes[:, g, 2 * h + c, 1, :].bitcast(FP8X4),
                        rhs_scale=mask_scales[:, g, 2 * h + c, 1, :],
                        start=(g == 0),
                        stop=(g == GROUPS - 1),
                    )

        def subtract_overlap(k):
            i, h = BLOCKS[k]
            d = work.tile([P, HALF], F32, name="d")
            minus_x[k] = d
            if k in s_squared_on_gpsimd:
                nc.vector.scalar_tensor_tensor(
                    out=d[:],
                    in0=overlaps[k][:],
                    scalar=area_col[:, i : i + 1],
                    in1=area_row[:, half_of(h)],
                    op0=ALU.subtract,
                    op1=ALU.subtract,
                )
            else:
                nc.vector.tensor_tensor(out=d[:], in0=area_row[:, half_of(h)], in1=overlaps[k][:], op=ALU.subtract)

        def square_s(k):
            i, h = BLOCKS[k]
            s2 = work.tile([P, HALF], F32, name="s2")
            s_squares[k] = s2
            if k in s_squared_on_gpsimd:
                nc.gpsimd.tensor_tensor(out=s2[:], in0=minus_x[k][:], in1=minus_x[k][:], op=ALU.mult)
            else:
                nc.scalar.activation(out=s2[:], in_=minus_x[k][:], func=ACT.Square, bias=area_col[:, i : i + 1])

        def invert_s(k):
            r = work.tile([P, HALF], F32, name="r")
            reciprocals[k] = r
            nc.scalar.activation(out=r[:], in_=s_squares[k][:], func=ACT.Abs_reciprocal_sqrt)

        def make_ratio(k):
            y = work.tile([P, HALF], F32, name="y")
            ratios[k] = y
            nc.vector.tensor_tensor(out=y[:], in0=overlaps[k][:], in1=reciprocals[k][:], op=ALU.mult)

        def square_ratio(k):
            y2 = work.tile([P, HALF], F32, name="y2")
            ratio_squares[k] = y2
            if k % 3 == 0 and k > 0:
                nc.vector.tensor_tensor(out=y2[:], in0=ratios[k][:], in1=ratios[k][:], op=ALU.mult)
            else:
                nc.scalar.activation(out=y2[:], in_=ratios[k][:], func=ACT.Square)

        def apply_gate(k):
            i, h = BLOCKS[k]
            engine = nc.gpsimd if k < 12 else nc.vector
            engine.tensor_tensor(
                out=gate[:, i, half_of(h)], in0=ratio_squares[k][:], in1=gate[:, i, half_of(h)], op=ALU.mult
            )

        def decay(i, h):
            e = work.tile([P, HALF], F32, name="e", bufs=4)
            nc.scalar.activation(out=e[:], in_=gate[:, i, half_of(h)], func=ACT.Exp, scale=-256.0)
            o = work.tile([P, HALF], F32, name="o", bufs=6)
            nc.vector.tensor_tensor(out=o[:], in0=e[:], in1=score_row[:, half_of(h)], op=ALU.mult)
            nc.sync.dma_start(out=out[i * P : (i + 1) * P, half_of(h)], in_=o[:])

        cast_feat(0, 0)
        cast_feat(0, 1)
        cast_feat(0, 2)
        cast_feat(0, 3)
        turn_ker(0)
        cast_feat(1, 0)
        cast_feat(1, 1)
        turn_feat(0, 0)
        copy_ker(0)
        cast_feat(1, 2)
        multiply_gains()
        cast_feat(1, 3)
        turn_feat(0, 1)
        cast_feat(2, 0)
        make_columns()
        cast_feat(2, 1)
        spread_score(0)
        scale_feat(0, 0)
        scale_feat(0, 1)
        turn_feat(1, 0)
        spread_score(1)
        quantise_ker(0)
        cast_feat(2, 2)
        copy_score(0)
        quantise_feat(0)
        turn_feat(1, 1)
        copy_score(1)
        make_gate(0)
        scale_feat(1, 0)
        make_logits(0)
        make_mask(0)
        cast_feat(2, 3)
        make_logits(1)
        turn_feat(2, 0)
        scale_feat(1, 1)
        make_gate(1)
        make_mask(1)
        quantise_feat(1)
        make_gate(2)
        turn_mask(0)
        turn_feat(2, 1)
        make_logits(2)
        scale_feat(2, 0)
        make_logits(3)
        scale_feat(2, 1)
        quantise_feat(2)
        square_mask(0)
        make_mask(2)
        make_gate(3)
        turn_mask(1)
        square_mask(1)
        turn_ker(1)
        turn_mask(2)
        copy_ker(1)
        make_mask(3)
        make_logits(4)
        make_mask(4)
        make_logits(5)
        weigh_mask(0)
        make_mask(5)
        quantise_ker(1)
        weigh_mask(1)
        square_mask(2)
        quantise_pair(1)
        turn_mask(3)
        units = len(UNITS)
        for k in range(2, units + 1):
            if k % 2 == 0 and k >= 4:
                make_gate(2 + k // 2)
            if k in (4, 5):
                copy_ker(k - 2)
            if k in (6, 7):
                quantise_ker(k - 4)
            if k in (3, 4):
                turn_ker(k - 1)
            sum_area(k - 2)
            if k in (14, 20):
                copy_area((k - 14) // 6)
            if k + 4 < units:
                make_logits(k + 4)
            if k in (8, 14):
                read_area((k - 8) // 6)
            if k + 3 < units:
                make_mask(k + 3)
            if k in (12, 18):
                spread_area((k - 12) // 6)
            if k + 2 < units:
                turn_mask(k + 2)
            if k >= units - 4:
                make_overlap(k - units + 4)
            if k >= units - 2:
                subtract_overlap(k - units + 2)
            if k < units:
                weigh_mask(k)
            if k >= 6:
                quantise_pair(k - 3)
            if k + 1 < units:
                square_mask(k + 1)
        quantise_pair(units - 2)
        quantise_pair(units - 1)
        make_gate(2 * TILES - 1)

        blocks = len(BLOCKS)
        for k in range(blocks + 4):
            if k == 0:
                sum_area(units - 1)
            if 5 <= k + 2 < blocks:
                make_overlap(k + 2)
            if 3 <= k + 1 < blocks:
                subtract_overlap(k + 1)
            for q in (2, 3):
                if k == q + 1:
                    read_area(q)
                if k == q + 2:
                    spread_area(q)
                if k == q + 3:
                    copy_area(q)
            if k < blocks:
                square_s(k)
            if 0 <= k - 1 < blocks:
                invert_s(k - 1)
            if 0 <= k - 2 < blocks:
                make_ratio(k - 2)
            if 0 <= k - 3 < blocks:
                square_ratio(k - 3)
            if 0 <= k - 4 < blocks:
                apply_gate(k - 4)
        for i in range(TILES):
            for h in range(2):
                decay(i, h)
